import numpy as np, ml_dtypes
CORES = [8,9,10,11,12,13]
N = 6
BF = ml_dtypes.bfloat16
def gentries(a):
    return np.ascontiguousarray(a.reshape(8, 16, -1).transpose(0, 2, 1)).reshape(8, -1)
def gtable(e):
    e = np.asarray(e); return np.ascontiguousarray(e.reshape(8, -1, 16).transpose(0, 2, 1)).reshape(128, -1).astype(np.int32)
def f(rng, *shape):
    return (rng.standard_normal(shape, dtype=np.float32) * np.exp2(rng.integers(-2, 3, shape[:-1] + (1,)))).astype(BF)
def wide(rng, *shape):
    v = f(rng, *shape).astype(np.float32); k = shape[:-2] + (1, shape[-1])
    return (v * np.exp2(rng.integers(-6, 7, k)) * (rng.random(k) > 0.0625)).astype(BF)
M, Q, V, TOP = 512, 256, 6, 15
def far_maps(rng):
    p = np.argsort(rng.random((N, 8, M)), axis=-1)
    return np.where(rng.random(p.shape) < 0.125, rng.integers(0, M, p.shape), p).astype(np.int32)
def lists(a):
    return np.stack([gtable(u) for u in a])
def setup_inputs(rng):
    return {"nx": far_maps(rng), "v": f(rng, N, 128, M), "x": lists(rng.integers(0, M, (N, 8, Q))), "e": lists(rng.integers(0, TOP + 1, (N, 8, V * Q)))}
def setup_inputs_ends(rng):
    d = setup_inputs(rng); k = rng.choice(np.array([0, TOP]), (N, 8, V, Q))
    k[:, :, :, 0] = 0; k[:, :, :, 1] = TOP; k[:, :, :, Q - 1] = 0; k[:, :, V - 1, Q - 1] = TOP
    d["e"] = lists(k.reshape(N, 8, V * Q))
    return d
def setup_inputs_still(rng):
    d = setup_inputs(rng); a = np.array(d["nx"]); s = int(rng.integers(0, 4)); p = np.arange(M)
    for r in range(N):
        h = (r + s) % 4; c = rng.choice(np.arange(2, M - 1), 8, replace=False)
        if h == 0:
            a[r] = p
        elif h == 1:
            c[0] = 0; c[1] = M - 1; a[r] = rng.permutation(c)[:, None]
        elif h == 2:
            c[0] = 1; c[1] = M - 1; a[r] = (p + rng.permutation(c)[:, None]) % M
        else:
            c[0] = 1; c[1] = M - 1; a[r] = p ^ rng.permutation(c)[:, None]
    d["nx"] = a; return d
def setup_inputs_alike(rng):
    d = setup_inputs(rng); k = rng.integers(0, TOP + 1, (N, 8, V, Q // 2))
    z = np.where((np.arange(N)[:, None] + np.arange(8)) % 2 == 0, M - 1, 0)
    d["x"] = lists(np.repeat(z[:, :, None], Q, axis=2)); d["e"] = lists(np.concatenate([k, k], -1).reshape(N, 8, V * Q)); return d
def setup_inputs_spread(rng):
    d = setup_inputs(rng)
    d["nx"] = np.floor(M * rng.random((N, 8, M)) ** 3).astype(np.int32)
    d["v"] = wide(rng, N, 128, M)
    d["x"] = lists(np.floor(M * rng.random((N, 8, Q)) ** 2)); d["e"] = lists(np.floor((TOP + 1) * rng.random((N, 8, V * Q)) ** 3)); return d
def check_inputs(d):
    bad = []
    for name, top in (("nx", M - 1), ("x", M - 1), ("e", TOP)):
        if np.min(d[name]) < 0 or np.max(d[name]) > top: bad.append("range of " + name)
    if not np.isfinite(d["v"].astype(np.float32)).all(): bad.append("finite v")
    return bad
def reference(nx, v, x, e):
    y = np.zeros((N, 128, Q), np.float32); g = np.arange(8)[:, None]; g3 = np.arange(8)[:, None, None]; i3 = np.arange(16)[None, :, None]
    for r in range(N):
        p = gentries(x[r]).astype(np.int64); k = gentries(e[r]).reshape(8, V, Q); s = np.zeros((8, 16, Q), np.float64)
        for t in range(V):
            q = (r + t) % N; vq = v[q].astype(np.float64).reshape(8, 16, M)
            for i in range(TOP):
                go = i < k[:, t]
                s = s + np.where(go[:, None, :], vq[g3, i3, p[:, None, :]], 0.0)
                p = np.where(go, nx[q][g, p], p)
        y[r] = s.reshape(128, Q).astype(np.float32)
    return {"y": y}

@@ -1,0 +1,397 @@
+import numpy as np
+from concourse.bass import DstId, RemoteDMATransfer
+from concourse.mybir import dt, AluOpType, AxisListType, ActivationFunctionType
+
+NR = 6
+NPOOL = 112
+SCRATCH = {
+    "nx8": ("sbuf", [128, 512], "int32"), "nx8b": ("sbuf", [128, 512], "bfloat16"),
+    "e128": ("sbuf", [128, 96], "int32"), "ebf": ("sbuf", [128, 96], "bfloat16"), "e8b": ("sbuf", [128, 1536], "bfloat16"),
+    "x128": ("sbuf", [128, 16], "int32"), "vbf": ("sbuf", [128, 512], "bfloat16"),
+    "ones": ("sbuf", [128, 144], "bfloat16"), "c256": ("sbuf", [128, 64], "bfloat16"),
+    "G8": ("sbuf", [128, 144], "bfloat16"), "G8a": ("sbuf", [128, 128], "bfloat16"), "G8b": ("sbuf", [128, 128], "bfloat16"),
+    "C8": ("sbuf", [128, 144], "bfloat16"), "SGt": ("sbuf", [128, 144], "bfloat16"), "SG": ("sbuf", [128, 144], "bfloat16"),
+    "CV": ("sbuf", [128, 144], "bfloat16"), "C2t": ("sbuf", [128, 144], "bfloat16"), "C2": ("sbuf", [128, 144], "bfloat16"),
+    "L16": ("sbuf", [128, 128], "bfloat16"), "bBt": ("sbuf", [128, 64], "bfloat16"), "bB": ("sbuf", [128, 64], "bfloat16"),
+    "bVt": ("sbuf", [128, 64], "bfloat16"), "bV": ("sbuf", [128, 64], "bfloat16"),
+    "IDN": ("sbuf", [128, 128], "bfloat16"), "vs1": ("sbuf", [128, 512], "bfloat16"),
+    "sel15": ("sbuf", [128, 128], "bfloat16"), "irow": ("sbuf", [128, 512], "bfloat16"),
+    "D2": ("sbuf", [128, 64], "float32"), "D4": ("sbuf", [128, 64], "float32"),
+    "pc": ("sbuf", [128, 2], "int32"), "ci": ("sbuf", [128, 2], "int32"), "bt": ("sbuf", [128, 3], "int32"),
+    "icol": ("sbuf", [128, 1], "float32"), "nicol": ("sbuf", [128, 1], "float32"), "n15": ("sbuf", [128, 1], "float32"),
+    "acol": ("sbuf", [128, 3], "float32"), "bcol": ("sbuf", [128, 3], "float32"),
+    "be": ("sbuf", [128, 96], "int32"), "de": ("sbuf", [128, 96], "float32"), "me": ("sbuf", [128, 96], "float32"),
+    "Ecat": ("sbuf", [128, 192], "bfloat16"),
+    "xf": ("sbuf", [128, 192], "float32"), "xi": ("sbuf", [128, 192], "uint16"),
+    "W": ("sbuf", [128, 512], "bfloat16"), "mabs": ("sbuf", [128, 512], "bfloat16"),
+    "mask": ("sbuf", [128, 1280], "bfloat16"),
+    "PT": ("sbuf", [128, 8192], "float32"), "P4": ("sbuf", [128, 512], "float32"),
+    "acc": ("sbuf", [128, 256], "float32"), "yb": ("sbuf", [128, 256], "float32"),
+}
+for _n in range(4):
+    SCRATCH["A%d" % _n] = ("sbuf", [128, 512], "bfloat16")
+    SCRATCH["B%d" % _n] = ("sbuf", [128, 512], "bfloat16")
+    if _n:
+        SCRATCH["U%d" % _n] = ("sbuf", [128, 512], "bfloat16")
+    SCRATCH["scl%d" % _n] = ("sbuf", [128, 64], "float32")
+    SCRATCH["lst%d" % _n] = ("sbuf", [128, 32], "uint16")
+for _n in range(1, 5):
+    SCRATCH["Wl%d" % _n] = ("sbuf", [128, 512], "bfloat16")
+for _n in range(6):
+    SCRATCH["r1_%d" % _n] = ("sbuf", [128, 256], "float32")
+for _n in range(5):
+    SCRATCH["pl%d" % _n] = ("sbuf", [128, 16], "uint16")
+    SCRATCH["R%d" % _n] = ("sbuf", [128, 256], "bfloat16")
+for _n in range(1, 6):
+    SCRATCH["scv%d" % _n] = ("sbuf", [128, 64], "float32")
+    SCRATCH["el%d" % _n] = ("sbuf", [128, 192], "bfloat16")
+    SCRATCH["ql%d" % _n] = ("sbuf", [128, 64], "float32")
+    SCRATCH["rr%d" % _n] = ("sbuf", [128, 256], "float32")
+    SCRATCH["rl%d" % _n] = ("sbuf", [128, 256], "float32")
+for _n in range(3):
+    SCRATCH["psE%d" % _n] = ("psum", [128, 512], "float32")
+    SCRATCH["psL%d" % _n] = ("psum", [128, 512], "float32")
+SCRATCH["psA"] = ("psum", [128, 512], "float32")
+SCRATCH["psB"] = ("psum", [128, 512], "float32")
+
+SEMAPHORES = (["s%d" % k for k in range(NPOOL)] + ["loc", "earr"] + ["w%d" % k for k in range(1, 5)]
+              + ["rq%d" % k for k in range(1, 6)] + ["rs%d" % k for k in range(1, 6)])
+
+
+def rank_program(g, core, T, topo):
+    rank = T.rank_of(core)
+    if rank is None:
+        return
+    queues = {"g": g, "v": g.vector, "s": g.scalar, "t": g.tensor, "y": g.sync}
+    ops = []
+    Op, AF = AluOpType, ActivationFunctionType
+
+    def add(q, calls, deps=(), rem=(), step=1):
+        if not isinstance(calls, list):
+            calls = [calls]
+        ops.append((q, calls, list(deps), list(rem), step))
+        return len(ops) - 1
+
+    V, S, P, Y = g.vector, g.scalar, g.tensor, g.sync
+
+    def vec(fn, *deps, rem=()):
+        return add("v", fn, deps, rem)
+
+    def sca(fn, *deps, rem=()):
+        return add("s", fn, deps, rem)
+
+    def pe(fns, *deps):
+        return add("t", fns, deps)
+
+    def gp(fn, *deps):
+        return add("g", fn, deps)
+
+    d_nx = add("y", lambda: Y.dma_start(T.nx8[0:8, :], T.nx[:, :]), step=16)
+    d_e = add("s", lambda: S.dma_start(T.e128[:, :], T.e[:, :]), step=16)
+    d_x = add("y", lambda: Y.dma_start(T.x128[:, :], T.x[:, :]), step=16)
+    d_v = add("s", lambda: S.dma_start(T.vbf[:, :], T.v[:, :]), step=16)
+
+    m1 = vec(lambda: V.memset(T.ones[:, :], 1.0))
+    m2 = vec(lambda: V.memset(T.c256[:, :], 256.0))
+    m8a = vec(lambda: V.memset(T.G8a[:, :], 0.0))
+    m8b = vec(lambda: V.memset(T.G8b[:, :], 0.0))
+    mc8 = vec(lambda: V.memset(T.C8[:, :], 0.0))
+    ms = vec(lambda: V.memset(T.sel15[0:1, :], 0.0))
+    ms = vec(lambda: V.memset(T.sel15[0:1, 15::16], 1.0), ms)
+    md2 = vec(lambda: V.memset(T.D2[:, :], 1.0))
+    md4 = vec(lambda: V.memset(T.D4[:, :], 1.0))
+    md2 = vec(lambda: V.memset(T.D2[:, 0::2], 0.0), md2)
+    md4 = vec(lambda: V.memset(T.D4[:, 0::4], 0.0), md4)
+    mc2 = vec(lambda: V.memset(T.C2[:, :], 0.0))
+    mcv = vec(lambda: V.memset(T.CV[:, :], 0.0))
+
+    k_pc = gp(lambda: g.iota(T.pc[:, :], [[1, 2]], 0, 1))
+    k_G8 = gp(lambda: g.affine_select(T.G8[0:8, :], T.ones[0:8, :], [[-1, 9], [0, 16]], Op.is_equal, 0.0, 0, 1), m1)
+    k_ir = gp(lambda: g.iota(T.irow[0:1, :], [[1, 512]], -256, 0, allow_small_or_imprecise_dtypes=True))
+    k_L16 = gp(lambda: g.affine_select(T.L16[0:16, :], T.ones[0:16, 0:128], [[0, 8], [-1, 16]], Op.is_equal, 0.0, 0, 1))
+    k_b1 = gp(lambda: g.affine_select(T.bBt[0:16, :], T.c256[0:16, :], [[0, 32], [-8, 2]], Op.is_ge, -2048.0, 0, 1), m2)
+    k_b2 = gp(lambda: g.affine_select(T.bB[0:16, :], T.bBt[0:16, :], [[0, 32], [8, 2]], Op.is_ge, -2048.0, 7, -1), k_b1)
+    k_c2 = gp(lambda: g.affine_select(T.C2t[:, :], T.ones[:, :], [[-16, 9], [0, 16]], Op.is_equal, 0.0, -7, 1))
+    k_I = gp(lambda: g.affine_select(T.IDN[:, :], T.ones[:, 0:128], [[-1, 128]], Op.is_equal, 0.0, 0, 1))
+    k_s1 = gp(lambda: g.affine_select(T.SGt[:, :], T.ones[:, :], [[-16, 9], [0, 16]], Op.is_ge, 0.0, 0, 1))
+    k_s2 = gp(lambda: g.affine_select(T.SG[:, :], T.SGt[:, :], [[16, 9], [0, 16]], Op.is_ge, 0.0, 15, -1), k_s1)
+    k_v1 = gp(lambda: g.affine_select(T.bVt[0:16, :], T.c256[0:16, :], [[0, 16], [-4, 4]], Op.is_ge, -2048.0, 0, 1))
+    k_bV = gp(lambda: g.affine_select(T.bV[0:16, :], T.bVt[0:16, :], [[0, 16], [4, 4]], Op.is_ge, -2048.0, 3, -1), k_v1)
+
+    v_ci = vec(lambda: V.tensor_scalar(T.ci[:, :], T.pc[:, :], 15, None, Op.bitwise_and), k_pc)
+    v_a = vec(lambda: V.tensor_copy(T.G8a[0:8, 1::2], T.G8[0:8, 1:128:2]), k_G8, m8a)
+    v_b = vec(lambda: V.tensor_copy(T.G8b[0:8, 0::2], T.G8[0:8, 0:128:2]), k_G8, m8b)
+    v_c8 = vec(lambda: V.tensor_copy(T.C8[0:8, 7::8], T.G8[0:8, 7::8]), k_G8, mc8)
+    v_a = vec(lambda: V.memset(T.G8a[0:8, 15::16], 0.0), v_a)
+    v_ic = vec(lambda: V.tensor_copy(T.icol[:, :], T.ci[:, 1:2]), v_ci)
+    v_ni = vec(lambda: V.tensor_scalar(T.nicol[:, :], T.ci[:, 1:2], -1.0, None, Op.mult), v_ci)
+    v_n15 = vec(lambda: V.tensor_scalar(T.n15[:, :], T.ci[:, 1:2], 1.0, None, Op.is_ge), v_ci)
+    v_bt = [vec(lambda n=n: V.tensor_scalar(T.bt[:, n - 1:n], T.ci[:, 0:1], n, 1, Op.logical_shift_right, Op.bitwise_and), v_ci)
+            for n in (1, 2, 3)]
+    v_ac = vec(lambda: V.tensor_scalar(T.acol[:, :], T.bt[:, :], T.n15[:, 0:1], None, Op.mult), v_n15, *v_bt)
+    v_bc = vec(lambda: V.tensor_scalar(T.bcol[:, :], T.acol[:, :], -1.0, 1.0, Op.mult, Op.add), v_ac)
+
+    use = [0]
+
+    def bias(rows, *deps):
+        b = T["psL%d" % (use[0] % 3)]
+        use[0] += 1
+        h = pe([lambda: P.matmul(b[:, 0:64], T.L16[0:16, :], rows[0:16, :], start=True, stop=False)], *deps)
+        return b, h
+
+    def extract(b, rows, cls, *deps):
+        n = len(cls)
+        return pe([lambda s=s: P.matmul(b[:, 0:64], cls[s], rows[:, s::n], start=False, stop=(s == n - 1))
+                   for s in range(n)], *deps)
+
+    def scan(scb, D, b, *deps):
+        return vec(lambda: V.tensor_tensor_scan(scb[:, :], D[:, :], b[:, 0:64], 0.0, Op.mult, Op.max), *deps)
+
+    def cvt(dst, scb, k, sc):
+        return vec(lambda: V.tensor_copy(dst[:, :], scb[:, k - 1::k]), sc)
+
+    c8s = [T.C8[0:8, 7 - s:135 - s] for s in range(8)]
+    c2s = [T.C2[:, 7 - s:135 - s] for s in range(8)]
+    cvs = [T.CV[:, 3 - s:131 - s] for s in range(4)]
+
+    v_nx = vec(lambda: V.tensor_scalar(T.nx8b[0:8, :], T.nx8[0:8, :], -256.0, None, Op.add), d_nx)
+    t_id = pe([lambda: P.matmul(T.psB[:, :], T.sel15[0:1, :], T.irow[0:1, :], start=True, stop=False)], ms, k_ir)
+    t_a = pe([lambda: P.matmul(T.psA[:, :], T.G8a[0:8, :], T.nx8b[0:8, :], start=True, stop=True)], v_nx, v_a)
+    t_b = pe([lambda: P.matmul(T.psB[:, :], T.G8b[0:8, :], T.nx8b[0:8, :], start=False, stop=True)], v_b)
+    b0, h0 = bias(T.bB, k_L16, k_b2)
+    t_l = extract(b0, T.nx8b[0:8, :], c8s, v_nx, v_c8)
+    s_P1 = sca(lambda: S.activation(T.PT[:, 512:1024], T.vbf[:, :], AF.Copy), d_v)
+    s_A0 = sca(lambda: S.activation(T.A0[:, :], T.psA[:, :], AF.Copy), t_a)
+
+    v_eb = vec(lambda: V.tensor_copy(T.ebf[:, :], T.e128[:, :]), d_e)
+    d_8 = add("y", lambda: Y.dma_start(T.e8b[0:8, :], T.ebf[:, :]), [v_eb], step=16)
+    v_e1 = vec(lambda: V.tensor_scalar(T.Ecat[:, 0:96], T.e128[:, :], 512.0, None, Op.mult), d_e)
+    v2 = vec(lambda: V.tensor_scalar(T.be[:, :], T.e128[:, :], 3, None, Op.bitwise_and), d_e)
+    v3 = vec(lambda: V.tensor_tensor(T.de[:, :], T.e128[:, :], T.be[:, :], Op.subtract), v2)
+    v4 = vec(lambda: V.tensor_scalar(T.me[:, :], T.be[:, :], 1.0, 512.0, Op.is_ge, Op.mult), v2)
+    v_e2 = vec(lambda: V.tensor_tensor(T.Ecat[:, 96:192], T.de[:, :], T.me[:, :], Op.mult), v3, v4)
+    v_x = vec(lambda: V.tensor_copy(T.pl0[:, :], T.x128[:, :]), d_x)
+    v_B0 = vec(lambda: V.tensor_copy(T.B0[:, :], T.psB[:, :]), t_b)
+
+    sc0 = scan(T.scl0, T.D2, b0, t_l, md2)
+    l_h = [cvt(T.lst0, T.scl0, 2, sc0)]
+    v_c2 = vec(lambda: V.tensor_copy(T.C2[:, 7::8], T.C2t[:, 7::8]), k_c2, mc2)
+
+    loc = [0]
+
+    def eng(d):
+        return len(topo.engines(core, d))
+
+    n_arr = eng([c for c in T.cores if c != core][0])
+
+    def send(dst_rank, out, in_, sem, deps):
+        d = T.cores[dst_rank]
+        rid, pid, _ = topo.addr(d)
+        loc[0] += eng(d)
+        add("g", lambda: g.remote_dma(out, in_, T.sem[sem], T.sem.loc, pid, rid, topo.mask(core, d)), deps, step=0)
+
+    def send_many(dst_ranks, outs, in_, sem, deps):
+        ds = [T.cores[r] for r in dst_ranks]
+        mask = topo.mask(core, ds[0])
+        ids = [DstId(rid=topo.addr(d)[0], pnc=topo.addr(d)[1]) for d in ds]
+        loc[0] += eng(ds[0])
+        add("g", lambda: g.remote_dma_fused([RemoteDMATransfer(dst_ids=ids, dma_engine_mask=mask, remote_sem=T.sem[sem],
+                                                               srcs=[in_], dsts=outs)], local_sem=T.sem.loc), deps, step=0)
+
+    send_many([(rank + t) % NR for t in range(1, NR)], [T["el%d" % t][:, :] for t in range(1, NR)], T.Ecat[:, :], "earr",
+              [v_e1, v_e2])
+
+    e_h = []
+
+    def e_block(u, n):
+        ps = T["psE%d" % u]
+        return pe([lambda i=i: P.matmul(ps[:, i:16 * n:16], T.G8[0:8, 0:128], T.e8b[0:8, 96 * i + 32 * u:96 * i + 32 * u + n],
+                                        start=True, stop=True) for i in range(16)], d_8, k_G8)
+
+    def e_mask(u, n, h):
+        return vec(lambda: V.tensor_scalar(T.mask[:, 512 * u:512 * u + 16 * n], T["psE%d" % u][:, 0:16 * n], T.icol[:, 0:1], None,
+                                           Op.is_equal), h, v_ic)
+
+    s_v1 = sca(lambda: S.activation(T.vs1[:, :], T.vbf[:, :].indirect(T.lst0[:, :]), AF.Copy), l_h[0], d_v)
+    s_z = sca(lambda: S.activation(T.PT[:, 0:512], T.vbf[:, :], AF.Copy, scale=0.0), d_v)
+
+    msk = [None] * 3
+    a_h, b_h = s_A0, v_B0
+    for n in range(4):
+        A, B, L = T["A%d" % n], T["B%d" % n], T["lst%d" % n]
+        U = T["U%d" % (n + 1)] if n < 3 else T.W
+        u_h = vec(lambda A=A, B=B, U=U, L=L: V.tensor_tensor(U[:, :], A[:, :].indirect(L[:, :]), B[:, :], Op.add), a_h, b_h, l_h[n])
+        if n == 3:
+            break
+        bb, hb = bias(T.bB)
+        tl = extract(bb, U, c2s, u_h, v_c2)
+        if n == 0:
+            t_P2 = pe([lambda: P.matmul(T.psA[:, :], T.IDN[:, :], T.vbf[:, :], start=True, stop=False)], k_I, s_A0, d_v)
+            t_P2 = pe([lambda: P.matmul(T.psA[:, :], T.IDN[:, :], T.vs1[:, :], start=False, stop=True)], s_v1)
+        A1, B1 = T["A%d" % (n + 1)], T["B%d" % (n + 1)]
+        a_h = vec(lambda U=U, A1=A1, n=n: V.tensor_scalar(A1[:, :], U[:, :], T.acol[:, n:n + 1], None, Op.mult), u_h, v_ac)
+        b_h = sca(lambda U=U, B1=B1, n=n: S.activation(B1[:, :], U[:, :], AF.Copy, scale=T.bcol[:, n:n + 1]), u_h, v_bc)
+        if n == 0:
+            s_P2 = sca(lambda: S.activation(T.PT[:, 1024:1536], T.psA[:, :], AF.Copy), t_P2)
+            v_cv = vec(lambda: V.tensor_copy(T.CV[:, 3::4], T.SG[:, 3::4]), k_s2, mcv)
+        e_h.append(e_block(n, 32 if n < 2 else 16))
+        if n == 1:
+            s_m = sca(lambda: S.activation(T.mabs[:, :], T.psE0[:, :], AF.Abs, bias=T.nicol[:, 0:1]), e_h[0], v_ni)
+            msk[0] = sca(lambda: S.activation(T.mask[:, 0:512], T.mabs[:, :], AF.Relu, bias=1.0, scale=-1.0), s_m)
+        sc = scan(T["scl%d" % (n + 1)], T.D2, bb, tl)
+        l_h.append(cvt(T["lst%d" % (n + 1)], T["scl%d" % (n + 1)], 2, sc))
+    w_h = u_h
+
+    for t in (1, 2, 3, 4):
+        send((rank - t) % NR, T["Wl%d" % t][:, :], T.W[:, :], "w%d" % t, [w_h])
+
+    pt_h = {0: s_z, 1: s_P1, 2: s_P2}
+
+    def slot(k):
+        if k == 16:
+            return T.P4[:, :]
+        return T.PT[:, 512 * k:512 * k + 512]
+
+    def build_add(k, frm, m, plus):
+        L = T["lst%d" % m]
+        pt_h[k] = vec(lambda: V.tensor_tensor(slot(k), slot(frm).indirect(L[:, :]), slot(plus), Op.add), pt_h[frm], pt_h[plus], l_h[m])
+
+    def build_move(k, frm, m):
+        L = T["lst%d" % m]
+        pt_h[k] = sca(lambda: S.activation(slot(k), slot(frm).indirect(L[:, :]), AF.Copy), pt_h[frm], l_h[m])
+
+    x_h = {}
+
+    def index(t):
+        c = 32 * t
+        if t == 0:
+            src, E, deps, rem = T.x128[:, :], T.Ecat, [d_x, v_e1, v_e2], []
+        else:
+            src, E = T["ql%d" % t][:, 3::4], T["el%d" % t]
+            deps, rem = [], [("earr", 5 * n_arr), ("rq%d" % t, n_arr)]
+        i1 = vec(lambda: V.tensor_tensor(T.xf[:, c:c + 16], src, E[:, 16 * t:16 * t + 16], Op.add), *deps, rem=rem)
+        i2 = vec(lambda: V.tensor_tensor(T.xf[:, c + 16:c + 32], src, E[:, 96 + 16 * t:112 + 16 * t], Op.add), *deps)
+        x_h[t] = vec(lambda: V.tensor_copy(T.xi[:, c:c + 32], T.xf[:, c:c + 32]), i1, i2)
+
+    p_h = {0: v_x}
+    build_move(5, 1, 2)
+    build_move(9, 1, 3)
+    build_move(13, 5, 3)
+    for t in range(5):
+        Wt = T.W if t == 0 else T["Wl%d" % t]
+        R, pl = T["R%d" % t], T["pl%d" % t]
+        r_h = vec(lambda R=R, Wt=Wt, pl=pl, t=t: V.tensor_tensor(R[:, :], Wt[:, :].indirect(pl[:, :]), T.mask[:, 256 * t:256 * t + 256],
+                                                                  Op.mult),
+                  w_h, p_h[t], msk[t // 2], rem=[("w%d" % t, n_arr)] if t else [])
+        bb, hb = bias(T.bV, k_bV)
+        tl = extract(bb, R, cvs, r_h, v_cv)
+        if t == 0:
+            build_move(6, 2, 2)
+            build_move(10, 2, 3)
+        elif t == 1:
+            msk[2] = e_mask(2, 16, e_h[2])
+            build_add(8, 4, 2, 16)
+        elif t == 2:
+            build_add(12, 8, 2, 4)
+            index(0)
+        elif t == 3:
+            index(1)
+        elif t == 4:
+            index(2)
+        scb = T["scv%d" % (t + 1)]
+        sc = scan(scb, T.D4, bb, tl, md4)
+        if t < 4:
+            p_h[t + 1] = cvt(T["pl%d" % (t + 1)], scb, 4, sc)
+        send((rank + t + 1) % NR, T["ql%d" % (t + 1)][:, :], scb[:, :], "rq%d" % (t + 1), [sc])
+        if t == 0:
+            msk[1] = e_mask(1, 32, e_h[1])
+            build_add(3, 1, 1, 2)
+            build_add(4, 3, 0, 1)
+            pt_h[16] = sca(lambda: S.activation(slot(16), slot(4), AF.Copy), pt_h[4])
+            build_move(14, 6, 3)
+            build_move(7, 3, 2)
+            build_move(11, 3, 3)
+            build_move(15, 7, 3)
+
+    all_pt = [pt_h[k] for k in range(16)]
+    r1 = {}
+
+    def first(t):
+        c, r = 32 * t, T["r1_%d" % t]
+        r1[t] = sca(lambda: S.activation(r[:, :], T.PT[:, :].indirect(T.xi[:, c:c + 16]), AF.Copy), x_h[t], *all_pt)
+
+    def second(t):
+        c, r = 32 * t, T["r1_%d" % t]
+        o = T["rr%d" % t] if t else T.acc
+        h = vec(lambda: V.tensor_tensor(o[:, :], T.PT[:, 0:6656].indirect(T.xi[:, c + 16:c + 32]), r[:, :], Op.add), r1[t], x_h[t])
+        if t:
+            send((rank - t) % NR, T["rl%d" % t][:, :], T["rr%d" % t][:, :], "rs%d" % t, [h])
+        return h
+
+    first(1)
+    first(2)
+    second(1)
+    index(3)
+    first(3)
+    second(2)
+    index(4)
+    first(4)
+    second(3)
+    first(0)
+    index(5)
+    first(5)
+    second(4)
+    second(5)
+    acc = second(0)
+    for t in range(1, 6):
+        o = T.psA[:, 0:256] if t < 5 else T.yb[:, :]
+        a = T.acc[:, :] if t == 1 else T.psA[:, 0:256]
+        acc = vec(lambda t=t, o=o, a=a: V.tensor_tensor(o, a, T["rl%d" % t][:, :], Op.add), acc, rem=[("rs%d" % t, n_arr)])
+    d_y = add("y", lambda: Y.dma_start(T.y[:, :], T.yb[:, :]), [acc], step=16)
+    add("y", [], [d_y])
+
+    known = {q: set() for q in queues}
+    seen_rem = {q: set() for q in queues}
+    waits, at_issue = [], []
+    for k, (q, calls, deps, rem, step) in enumerate(ops):
+        w = []
+        for d in deps:
+            if d not in known[q]:
+                w.append(d)
+                known[q] |= at_issue[d]
+                known[q].add(d)
+        w = [d for d in w if not any(d in at_issue[o] for o in w if o != d)]
+        waits.append(w)
+        at_issue.append(set(known[q]))
+    wanted = set(d for w in waits for d in w)
+    count, last, sem_of, owner = {}, {}, {}, {}
+    free = list(range(NPOOL))
+    for k, (q, calls, deps, rem, step) in enumerate(ops):
+        eq = queues[q]
+        for d in waits[k]:
+            eq.wait_ge(T.sem["s%d" % sem_of[d][0]], sem_of[d][1])
+        for name, val in rem:
+            if name not in seen_rem[q]:
+                eq.wait_ge(T.sem[name], val)
+                seen_rem[q].add(name)
+        if k in wanted:
+            s = None
+            if step == 1:
+                for c in owner.get(q, []):
+                    if last[c] in at_issue[k]:
+                        s = c
+                        break
+            if s is None:
+                s = free.pop(0)
+                count[s] = 0
+                if step == 1:
+                    owner.setdefault(q, []).append(s)
+            for fn in calls:
+                fn().then_inc(T.sem["s%d" % s], step)
+                count[s] += step
+            last[s] = k
+            sem_of[k] = (s, count[s])
+        else:
+            for fn in calls:
+                fn()
+    g.wait_ge(T.sem.loc, loc[0])

@@ -3,56 +3,27 @@ from concourse.bass import DstId, RemoteDMATransfer
 from concourse.mybir import dt, AluOpType, AxisListType, ActivationFunctionType
 
 NR = 6
-NPOOL = 112
-SCRATCH = {
-    "nx8": ("sbuf", [128, 512], "int32"), "nx8b": ("sbuf", [128, 512], "bfloat16"),
-    "e128": ("sbuf", [128, 96], "int32"), "ebf": ("sbuf", [128, 96], "bfloat16"), "e8b": ("sbuf", [128, 1536], "bfloat16"),
-    "x128": ("sbuf", [128, 16], "int32"), "vbf": ("sbuf", [128, 512], "bfloat16"),
-    "ones": ("sbuf", [128, 144], "bfloat16"), "c256": ("sbuf", [128, 64], "bfloat16"),
-    "G8": ("sbuf", [128, 144], "bfloat16"), "G8a": ("sbuf", [128, 128], "bfloat16"), "G8b": ("sbuf", [128, 128], "bfloat16"),
-    "C8": ("sbuf", [128, 144], "bfloat16"), "SGt": ("sbuf", [128, 144], "bfloat16"), "SG": ("sbuf", [128, 144], "bfloat16"),
-    "CV": ("sbuf", [128, 144], "bfloat16"), "C2t": ("sbuf", [128, 144], "bfloat16"), "C2": ("sbuf", [128, 144], "bfloat16"),
-    "L16": ("sbuf", [128, 128], "bfloat16"), "bBt": ("sbuf", [128, 64], "bfloat16"), "bB": ("sbuf", [128, 64], "bfloat16"),
-    "bVt": ("sbuf", [128, 64], "bfloat16"), "bV": ("sbuf", [128, 64], "bfloat16"),
-    "IDN": ("sbuf", [128, 128], "bfloat16"), "vs1": ("sbuf", [128, 512], "bfloat16"),
-    "sel15": ("sbuf", [128, 128], "bfloat16"), "irow": ("sbuf", [128, 512], "bfloat16"),
-    "D2": ("sbuf", [128, 64], "float32"), "D4": ("sbuf", [128, 64], "float32"),
-    "pc": ("sbuf", [128, 2], "int32"), "ci": ("sbuf", [128, 2], "int32"), "bt": ("sbuf", [128, 3], "int32"),
-    "icol": ("sbuf", [128, 1], "float32"), "nicol": ("sbuf", [128, 1], "float32"), "n15": ("sbuf", [128, 1], "float32"),
-    "acol": ("sbuf", [128, 3], "float32"), "bcol": ("sbuf", [128, 3], "float32"),
-    "be": ("sbuf", [128, 96], "int32"), "de": ("sbuf", [128, 96], "float32"), "me": ("sbuf", [128, 96], "float32"),
-    "Ecat": ("sbuf", [128, 192], "bfloat16"),
-    "xf": ("sbuf", [128, 192], "float32"), "xi": ("sbuf", [128, 192], "uint16"),
-    "W": ("sbuf", [128, 512], "bfloat16"), "mabs": ("sbuf", [128, 512], "bfloat16"),
-    "mask": ("sbuf", [128, 1280], "bfloat16"),
-    "PT": ("sbuf", [128, 8192], "float32"), "P4": ("sbuf", [128, 512], "float32"),
-    "acc": ("sbuf", [128, 256], "float32"), "yb": ("sbuf", [128, 256], "float32"),
-}
-for _n in range(4):
-    SCRATCH["A%d" % _n] = ("sbuf", [128, 512], "bfloat16")
-    SCRATCH["B%d" % _n] = ("sbuf", [128, 512], "bfloat16")
-    if _n:
-        SCRATCH["U%d" % _n] = ("sbuf", [128, 512], "bfloat16")
-    SCRATCH["scl%d" % _n] = ("sbuf", [128, 64], "float32")
-    SCRATCH["lst%d" % _n] = ("sbuf", [128, 32], "uint16")
-for _n in range(1, 5):
-    SCRATCH["Wl%d" % _n] = ("sbuf", [128, 512], "bfloat16")
+NPOOL = 110
+BF, F32, I32, U16 = "bfloat16", "float32", "int32", "uint16"
+SCRATCH = {}
+for _n, _c, _d in (("nx32", 128, I32), ("nxb", 128, BF), ("nxl", 32, I32), ("nxt", 32, I32), ("e128", 96, I32), ("ebf", 96, BF),
+                   ("e32b", 384, BF), ("x128", 16, I32), ("vbf", 512, BF), ("ones", 512, BF), ("c256", 64, BF), ("G32", 512, BF),
+                   ("Gb", 512, BF), ("CV", 144, BF), ("C7t", 144, BF), ("C7", 144, BF), ("L16", 128, BF), ("bVt", 64, BF),
+                   ("bV", 64, BF), ("IDN", 128, BF), ("D4", 64, F32), ("pc", 2, I32), ("ci", 2, I32), ("bt", 4, I32),
+                   ("icol", 1, F32), ("n15", 1, F32), ("acol", 4, F32), ("bcol", 4, F32), ("EL", 96, I32), ("ea", 96, I32),
+                   ("E1", 96, F32), ("E2", 96, F32), ("QL", 384, F32), ("xf1", 96, F32), ("xi1", 96, U16), ("xf2", 96, F32),
+                   ("xi2", 96, U16), ("W", 512, BF), ("mask", 1280, BF), ("TT", 9728, F32), ("P4", 512, F32), ("yb", 256, F32)):
+    SCRATCH[_n] = ("sbuf", [128, _c], _d)
 for _n in range(6):
-    SCRATCH["r1_%d" % _n] = ("sbuf", [128, 256], "float32")
-for _n in range(5):
-    SCRATCH["pl%d" % _n] = ("sbuf", [128, 16], "uint16")
-    SCRATCH["R%d" % _n] = ("sbuf", [128, 256], "bfloat16")
-for _n in range(1, 6):
-    SCRATCH["scv%d" % _n] = ("sbuf", [128, 64], "float32")
-    SCRATCH["el%d" % _n] = ("sbuf", [128, 192], "bfloat16")
-    SCRATCH["ql%d" % _n] = ("sbuf", [128, 64], "float32")
-    SCRATCH["rr%d" % _n] = ("sbuf", [128, 256], "float32")
-    SCRATCH["rl%d" % _n] = ("sbuf", [128, 256], "float32")
-for _n in range(3):
-    SCRATCH["psE%d" % _n] = ("psum", [128, 512], "float32")
-    SCRATCH["psL%d" % _n] = ("psum", [128, 512], "float32")
-SCRATCH["psA"] = ("psum", [128, 512], "float32")
-SCRATCH["psB"] = ("psum", [128, 512], "float32")
+    for _b, _c, _d, _k in (("A", 512, BF, (0, 1, 2, 3)), ("B", 512, BF, (0, 1, 2, 3)), ("U", 512, BF, (1, 2, 3)),
+                           ("vs", 512, BF, (1, 2, 3)), ("scl", 128, F32, (1, 2, 3)), ("lst", 32, U16, (0, 1, 2, 3)),
+                           ("Wl", 512, BF, (1, 2, 3, 4)), ("r1_", 256, F32, range(6)), ("rr", 256, F32, range(6)),
+                           ("pl", 16, U16, range(5)), ("R", 256, BF, range(5)), ("scv", 64, F32, range(1, 6)),
+                           ("rl", 256, F32, range(1, 6))):
+        if _n in _k:
+            SCRATCH["%s%d" % (_b, _n)] = ("sbuf", [128, _c], _d)
+for _n in ("psL0", "psL1", "psL2", "psL3", "psE0", "psE1", "psE2", "psT"):
+    SCRATCH[_n] = ("psum", [128, 512], F32)
 
 SEMAPHORES = (["s%d" % k for k in range(NPOOL)] + ["loc", "earr"] + ["w%d" % k for k in range(1, 5)]
               + ["rq%d" % k for k in range(1, 6)] + ["rs%d" % k for k in range(1, 6)])
@@ -86,96 +57,81 @@ def rank_program(g, core, T, topo):
     def gp(fn, *deps):
         return add("g", fn, deps)
 
-    d_nx = add("y", lambda: Y.dma_start(T.nx8[0:8, :], T.nx[:, :]), step=16)
+    d_nx = add("y", lambda: Y.dma_start(T.nx32[0:32, :], T.nx[:, :]), step=16)
+    d_l = [add("s", lambda: S.dma_start(T.nxl[:, 0:16], T.nx[0::2, :]), step=16),
+           add("y", lambda: Y.dma_start(T.nxl[:, 16:32], T.nx[1::2, :]), step=16)]
     d_e = add("s", lambda: S.dma_start(T.e128[:, :], T.e[:, :]), step=16)
-    d_x = add("y", lambda: Y.dma_start(T.x128[:, :], T.x[:, :]), step=16)
     d_v = add("s", lambda: S.dma_start(T.vbf[:, :], T.v[:, :]), step=16)
+    d_e0 = add("y", lambda: Y.dma_start(T.EL[:, 0:16], T.e[:, 0:16]), step=16)
+    d_x = add("y", lambda: Y.dma_start(T.x128[:, :], T.x[:, :]), step=16)
 
     m1 = vec(lambda: V.memset(T.ones[:, :], 1.0))
     m2 = vec(lambda: V.memset(T.c256[:, :], 256.0))
-    m8a = vec(lambda: V.memset(T.G8a[:, :], 0.0))
-    m8b = vec(lambda: V.memset(T.G8b[:, :], 0.0))
-    mc8 = vec(lambda: V.memset(T.C8[:, :], 0.0))
-    ms = vec(lambda: V.memset(T.sel15[0:1, :], 0.0))
-    ms = vec(lambda: V.memset(T.sel15[0:1, 15::16], 1.0), ms)
-    md2 = vec(lambda: V.memset(T.D2[:, :], 1.0))
-    md4 = vec(lambda: V.memset(T.D4[:, :], 1.0))
-    md2 = vec(lambda: V.memset(T.D2[:, 0::2], 0.0), md2)
-    md4 = vec(lambda: V.memset(T.D4[:, 0::4], 0.0), md4)
-    mc2 = vec(lambda: V.memset(T.C2[:, :], 0.0))
-    mcv = vec(lambda: V.memset(T.CV[:, :], 0.0))
-
+    m_b = vec(lambda: V.memset(T.Gb[:, :], 0.0))
+    m_n = vec(lambda: V.memset(T.nxb[:, :], 0.0))
+    m_bs = [vec(lambda: V.memset(T.Gb[32:33, 15::16], 1.0), m_b)]
+    for q in (0, 1, 3):
+        m_bs.append(vec(lambda q=q: V.memset(T.Gb[64:65, 128 * q + 15:128 * q + 128:16], 128.0 * q - 256.0), m_b))
+    m_n1 = vec(lambda: V.memset(T.nxb[64:65, :], 1.0), m_n)
+    m_n2 = vec(lambda: V.tensor_tensor_scan(T.nxb[32:33, :], T.ones[32:33, 0:128], T.ones[32:33, 0:128], -1.0, Op.mult, Op.add),
+               m_n, m1)
     k_pc = gp(lambda: g.iota(T.pc[:, :], [[1, 2]], 0, 1))
-    k_G8 = gp(lambda: g.affine_select(T.G8[0:8, :], T.ones[0:8, :], [[-1, 9], [0, 16]], Op.is_equal, 0.0, 0, 1), m1)
-    k_ir = gp(lambda: g.iota(T.irow[0:1, :], [[1, 512]], -256, 0, allow_small_or_imprecise_dtypes=True))
+    k_G = gp(lambda: g.affine_select(T.G32[0:32, :], T.ones[0:32, :], [[-1, 4], [-4, 8], [0, 16]], Op.is_equal, 0.0, 0, 1), m1)
+    k_c7 = gp(lambda: g.affine_select(T.C7t[:, :], T.ones[:, 0:144], [[-16, 9], [0, 16]], Op.is_equal, 0.0, -7, 1))
     k_L16 = gp(lambda: g.affine_select(T.L16[0:16, :], T.ones[0:16, 0:128], [[0, 8], [-1, 16]], Op.is_equal, 0.0, 0, 1))
-    k_b1 = gp(lambda: g.affine_select(T.bBt[0:16, :], T.c256[0:16, :], [[0, 32], [-8, 2]], Op.is_ge, -2048.0, 0, 1), m2)
-    k_b2 = gp(lambda: g.affine_select(T.bB[0:16, :], T.bBt[0:16, :], [[0, 32], [8, 2]], Op.is_ge, -2048.0, 7, -1), k_b1)
-    k_c2 = gp(lambda: g.affine_select(T.C2t[:, :], T.ones[:, :], [[-16, 9], [0, 16]], Op.is_equal, 0.0, -7, 1))
     k_I = gp(lambda: g.affine_select(T.IDN[:, :], T.ones[:, 0:128], [[-1, 128]], Op.is_equal, 0.0, 0, 1))
-    k_s1 = gp(lambda: g.affine_select(T.SGt[:, :], T.ones[:, :], [[-16, 9], [0, 16]], Op.is_ge, 0.0, 0, 1))
-    k_s2 = gp(lambda: g.affine_select(T.SG[:, :], T.SGt[:, :], [[16, 9], [0, 16]], Op.is_ge, 0.0, 15, -1), k_s1)
-    k_v1 = gp(lambda: g.affine_select(T.bVt[0:16, :], T.c256[0:16, :], [[0, 16], [-4, 4]], Op.is_ge, -2048.0, 0, 1))
+    k_v1 = gp(lambda: g.affine_select(T.bVt[0:16, :], T.c256[0:16, :], [[0, 16], [-4, 4]], Op.is_ge, -2048.0, 0, 1), m2)
     k_bV = gp(lambda: g.affine_select(T.bV[0:16, :], T.bVt[0:16, :], [[0, 16], [4, 4]], Op.is_ge, -2048.0, 3, -1), k_v1)
+    t_cv = pe([lambda: P.matmul(T.psL3[:, 0:128], T.G32[0:32, 0:128], T.G32[0:32, 0:128], start=True, stop=True)], k_G)
 
+    def slot(k):
+        return T.TT[:, 512 * k:512 * k + 512]
+
+    def pt(e):
+        return slot(3 + e)
+
+    z_h = [sca(lambda a=a: S.activation(pt(4 * a), T.ones[:, :], AF.Copy, scale=0.0), m1) for a in range(4)]
     v_ci = vec(lambda: V.tensor_scalar(T.ci[:, :], T.pc[:, :], 15, None, Op.bitwise_and), k_pc)
-    v_a = vec(lambda: V.tensor_copy(T.G8a[0:8, 1::2], T.G8[0:8, 1:128:2]), k_G8, m8a)
-    v_b = vec(lambda: V.tensor_copy(T.G8b[0:8, 0::2], T.G8[0:8, 0:128:2]), k_G8, m8b)
-    v_c8 = vec(lambda: V.tensor_copy(T.C8[0:8, 7::8], T.G8[0:8, 7::8]), k_G8, mc8)
-    v_a = vec(lambda: V.memset(T.G8a[0:8, 15::16], 0.0), v_a)
-    v_ic = vec(lambda: V.tensor_copy(T.icol[:, :], T.ci[:, 1:2]), v_ci)
-    v_ni = vec(lambda: V.tensor_scalar(T.nicol[:, :], T.ci[:, 1:2], -1.0, None, Op.mult), v_ci)
     v_n15 = vec(lambda: V.tensor_scalar(T.n15[:, :], T.ci[:, 1:2], 1.0, None, Op.is_ge), v_ci)
-    v_bt = [vec(lambda n=n: V.tensor_scalar(T.bt[:, n - 1:n], T.ci[:, 0:1], n, 1, Op.logical_shift_right, Op.bitwise_and), v_ci)
-            for n in (1, 2, 3)]
+    v_bt = [vec(lambda n=n: V.tensor_scalar(T.bt[:, n:n + 1], T.ci[:, 0:1], n, 1, Op.logical_shift_right, Op.bitwise_and), v_ci)
+            for n in range(4)]
+    md4 = vec(lambda: V.memset(T.D4[:, :], 1.0))
+    mc7 = vec(lambda: V.memset(T.C7[:, :], 0.0))
+    mcv = vec(lambda: V.memset(T.CV[:, :], 0.0))
+    md4 = vec(lambda: V.memset(T.D4[:, 0::4], 0.0), md4)
     v_ac = vec(lambda: V.tensor_scalar(T.acol[:, :], T.bt[:, :], T.n15[:, 0:1], None, Op.mult), v_n15, *v_bt)
-    v_bc = vec(lambda: V.tensor_scalar(T.bcol[:, :], T.acol[:, :], -1.0, 1.0, Op.mult, Op.add), v_ac)
+    v_b = vec(lambda: V.tensor_copy(T.Gb[0:32, :], T.G32[0:32, :]), k_G, m_b)
+    v_b = vec(lambda: V.memset(T.Gb[0:32, 15::16], 0.0), v_b)
+    v_bc = sca(lambda: S.activation(T.bcol[:, :], T.acol[:, :], AF.Copy, bias=1.0, scale=-1.0), v_ac)
 
-    use = [0]
-
-    def bias(rows, *deps):
-        b = T["psL%d" % (use[0] % 3)]
-        use[0] += 1
-        h = pe([lambda: P.matmul(b[:, 0:64], T.L16[0:16, :], rows[0:16, :], start=True, stop=False)], *deps)
-        return b, h
-
-    def extract(b, rows, cls, *deps):
-        n = len(cls)
-        return pe([lambda s=s: P.matmul(b[:, 0:64], cls[s], rows[:, s::n], start=False, stop=(s == n - 1))
-                   for s in range(n)], *deps)
-
-    def scan(scb, D, b, *deps):
-        return vec(lambda: V.tensor_tensor_scan(scb[:, :], D[:, :], b[:, 0:64], 0.0, Op.mult, Op.max), *deps)
-
-    def cvt(dst, scb, k, sc):
-        return vec(lambda: V.tensor_copy(dst[:, :], scb[:, k - 1::k]), sc)
-
-    c8s = [T.C8[0:8, 7 - s:135 - s] for s in range(8)]
-    c2s = [T.C2[:, 7 - s:135 - s] for s in range(8)]
+    c7s = [T.C7[:, 3 - s:131 - s] for s in range(4)]
     cvs = [T.CV[:, 3 - s:131 - s] for s in range(4)]
 
-    v_nx = vec(lambda: V.tensor_scalar(T.nx8b[0:8, :], T.nx8[0:8, :], -256.0, None, Op.add), d_nx)
-    t_id = pe([lambda: P.matmul(T.psB[:, :], T.sel15[0:1, :], T.irow[0:1, :], start=True, stop=False)], ms, k_ir)
-    t_a = pe([lambda: P.matmul(T.psA[:, :], T.G8a[0:8, :], T.nx8b[0:8, :], start=True, stop=True)], v_nx, v_a)
-    t_b = pe([lambda: P.matmul(T.psB[:, :], T.G8b[0:8, :], T.nx8b[0:8, :], start=False, stop=True)], v_b)
-    b0, h0 = bias(T.bB, k_L16, k_b2)
-    t_l = extract(b0, T.nx8b[0:8, :], c8s, v_nx, v_c8)
-    s_P1 = sca(lambda: S.activation(T.PT[:, 512:1024], T.vbf[:, :], AF.Copy), d_v)
-    s_A0 = sca(lambda: S.activation(T.A0[:, :], T.psA[:, :], AF.Copy), t_a)
+    def bias(k, *deps):
+        b = T["psL%d" % k]
+        pe([lambda: P.matmul(b[:, 0:64], T.L16[0:16, :], T.bV[0:16, :], start=True, stop=False)], *deps)
 
+    def extract(k, rows, cls, *deps):
+        b = T["psL%d" % k]
+        return pe([lambda s=s: P.matmul(b[:, 0:64], cls[s], rows[:, s::4], start=False, stop=(s == 3)) for s in range(4)], *deps)
+
+    def scan(out, k, *deps):
+        return vec(lambda: V.tensor_tensor_scan(out, T.D4[:, :], T["psL%d" % k][:, 0:64], 0.0, Op.mult, Op.max), *deps)
+
+    v_nx = vec(lambda: V.tensor_scalar(T.nxb[0:32, :], T.nx32[0:32, :], -256.0, None, Op.add), d_nx, m_n)
+    t_0 = [pe([lambda q=q: P.matmul(T["psE%d" % (q // 2)][:, 128 * (q % 2):128 * (q % 2) + 128], T.Gb[0:65, 128 * q:128 * q + 128],
+                                    T.nxb[0:65, :], start=True, stop=True) for q in (2 * h, 2 * h + 1)],
+              v_nx, v_b, m_n1, m_n2, *m_bs) for h in (0, 1)]
+    v_tr = vec(lambda: V.transpose(T.nxt[:, :], T.nxl[:, :]), *d_l)
+    v_l0 = vec(lambda: V.tensor_copy(T.lst0[:, :], T.nxt[:, :]), v_tr)
+    s_A0 = sca(lambda: S.activation(T.A0[:, 0:256], T.psE0[:, 0:256], AF.Copy, scale=T.acol[:, 0:1]), t_0[0], v_ac)
     v_eb = vec(lambda: V.tensor_copy(T.ebf[:, :], T.e128[:, :]), d_e)
-    d_8 = add("y", lambda: Y.dma_start(T.e8b[0:8, :], T.ebf[:, :]), [v_eb], step=16)
-    v_e1 = vec(lambda: V.tensor_scalar(T.Ecat[:, 0:96], T.e128[:, :], 512.0, None, Op.mult), d_e)
-    v2 = vec(lambda: V.tensor_scalar(T.be[:, :], T.e128[:, :], 3, None, Op.bitwise_and), d_e)
-    v3 = vec(lambda: V.tensor_tensor(T.de[:, :], T.e128[:, :], T.be[:, :], Op.subtract), v2)
-    v4 = vec(lambda: V.tensor_scalar(T.me[:, :], T.be[:, :], 1.0, 512.0, Op.is_ge, Op.mult), v2)
-    v_e2 = vec(lambda: V.tensor_tensor(T.Ecat[:, 96:192], T.de[:, :], T.me[:, :], Op.mult), v3, v4)
-    v_x = vec(lambda: V.tensor_copy(T.pl0[:, :], T.x128[:, :]), d_x)
-    v_B0 = vec(lambda: V.tensor_copy(T.B0[:, :], T.psB[:, :]), t_b)
-
-    sc0 = scan(T.scl0, T.D2, b0, t_l, md2)
-    l_h = [cvt(T.lst0, T.scl0, 2, sc0)]
-    v_c2 = vec(lambda: V.tensor_copy(T.C2[:, 7::8], T.C2t[:, 7::8]), k_c2, mc2)
+    d_8 = add("y", lambda: Y.dma_start(T.e32b[0:32, :], T.ebf[:, :]), [v_eb], step=16)
+    v_A0 = vec(lambda: V.tensor_scalar(T.A0[:, 256:512], T.psE1[:, 0:256], T.acol[:, 0:1], None, Op.mult), t_0[1], v_ac)
+    v_B0 = vec(lambda: V.tensor_scalar(T.B0[:, 0:256], T.psE0[:, 0:256], T.bcol[:, 0:1], None, Op.mult), s_A0, v_bc)
+    s_B0 = sca(lambda: S.activation(T.B0[:, 256:512], T.psE1[:, 0:256], AF.Copy, scale=T.bcol[:, 0:1]), v_A0, v_bc)
+    v_c7 = sca(lambda: S.activation(T.C7[:, 3::4], T.C7t[:, 3::4], AF.Copy), k_c7, mc7)
+    v_cv = sca(lambda: S.activation(T.CV[:, 3:128:4], T.psL3[:, 3:128:4], AF.Copy), t_cv, mcv)
 
     loc = [0]
 
@@ -190,163 +146,194 @@ def rank_program(g, core, T, topo):
         loc[0] += eng(d)
         add("g", lambda: g.remote_dma(out, in_, T.sem[sem], T.sem.loc, pid, rid, topo.mask(core, d)), deps, step=0)
 
-    def send_many(dst_ranks, outs, in_, sem, deps):
-        ds = [T.cores[r] for r in dst_ranks]
-        mask = topo.mask(core, ds[0])
-        ids = [DstId(rid=topo.addr(d)[0], pnc=topo.addr(d)[1]) for d in ds]
-        loc[0] += eng(ds[0])
-        add("g", lambda: g.remote_dma_fused([RemoteDMATransfer(dst_ids=ids, dma_engine_mask=mask, remote_sem=T.sem[sem],
-                                                               srcs=[in_], dsts=outs)], local_sem=T.sem.loc), deps, step=0)
+    parts, es = [], topo.engines(core, [c for c in T.cores if c != core][0])
+    for t in range(1, NR):
+        d, n = T.cores[(rank + t) % NR], len(es) // (4 if t < 4 else 8)
+        o = sum(p[1] for p in parts)
+        parts.append((RemoteDMATransfer(dst_ids=[DstId(rid=topo.addr(d)[0], pnc=topo.addr(d)[1])],
+                                        dma_engine_mask=sum(1 << x for x in es[o:o + n]), remote_sem=T.sem["earr"],
+                                        srcs=[T.e128[:, 16 * t:16 * t + 16]], dsts=[T.EL[:, 16 * t:16 * t + 16]]), n))
+    loc[0] += n_arr
+    add("g", lambda: g.remote_dma_fused([p[0] for p in parts], local_sem=T.sem.loc), [d_e], step=0)
 
-    send_many([(rank + t) % NR for t in range(1, NR)], [T["el%d" % t][:, :] for t in range(1, NR)], T.Ecat[:, :], "earr",
-              [v_e1, v_e2])
+    s_v1 = sca(lambda: S.activation(T.vs1[:, :], T.vbf[:, :].indirect(T.lst0[:, :]), AF.Copy), v_l0, d_v)
+    sums = {2: T.psT, 3: T.psE2, 4: T.psT}
+    vs = [T.vbf, T.vs1, T.vs2, T.vs3]
 
+    def plus(k, i, *deps):
+        return pe([lambda: P.matmul(sums[k][:, :], T.IDN[:, :], vs[i][:, :], start=(i == 0), stop=(i == k - 1))], *deps)
+
+    plus(2, 0, k_I, d_v)
+    plus(3, 0)
+    bias(0, k_L16, k_bV)
+    bias(1)
+    l_h = [v_l0]
+    a_h, b_h = [s_A0, v_A0], [v_B0, s_B0]
     e_h = []
 
-    def e_block(u, n):
-        ps = T["psE%d" % u]
-        return pe([lambda i=i: P.matmul(ps[:, i:16 * n:16], T.G8[0:8, 0:128], T.e8b[0:8, 96 * i + 32 * u:96 * i + 32 * u + n],
-                                        start=True, stop=True) for i in range(16)], d_8, k_G8)
+    def e_block(u, lo, hi, *deps):
+        ps, w = T["psE%d" % u], 32 if u < 2 else 16
+        e_h.append(pe([lambda i=i: P.matmul(ps[:, i:16 * w:16], T.G32[0:32, 128 * (i // 4):128 * (i // 4) + 128],
+                                            T.e32b[0:32, 96 * (i % 4) + 32 * u:96 * (i % 4) + 32 * u + w], start=True, stop=True)
+                       for i in range(lo, hi)], d_8, k_G, s_B0, v_B0, *deps))
 
-    def e_mask(u, n, h):
-        return vec(lambda: V.tensor_scalar(T.mask[:, 512 * u:512 * u + 16 * n], T["psE%d" % u][:, 0:16 * n], T.icol[:, 0:1], None,
-                                           Op.is_equal), h, v_ic)
-
-    s_v1 = sca(lambda: S.activation(T.vs1[:, :], T.vbf[:, :].indirect(T.lst0[:, :]), AF.Copy), l_h[0], d_v)
-    s_z = sca(lambda: S.activation(T.PT[:, 0:512], T.vbf[:, :], AF.Copy, scale=0.0), d_v)
-
-    msk = [None] * 3
-    a_h, b_h = s_A0, v_B0
     for n in range(4):
         A, B, L = T["A%d" % n], T["B%d" % n], T["lst%d" % n]
         U = T["U%d" % (n + 1)] if n < 3 else T.W
-        u_h = vec(lambda A=A, B=B, U=U, L=L: V.tensor_tensor(U[:, :], A[:, :].indirect(L[:, :]), B[:, :], Op.add), a_h, b_h, l_h[n])
+        k = 2 * (n % 2)
+        u_h = [vec(lambda A=A, B=B, U=U, L=L, h=h: V.tensor_tensor(U[:, 256 * h:256 * h + 256],
+                                                                  A[:, :].indirect(L[:, 16 * h:16 * h + 16]),
+                                                                  B[:, 256 * h:256 * h + 256], Op.add),
+                   *a_h, b_h[h], l_h[n]) for h in (0, 1)]
         if n == 3:
             break
-        bb, hb = bias(T.bB)
-        tl = extract(bb, U, c2s, u_h, v_c2)
-        if n == 0:
-            t_P2 = pe([lambda: P.matmul(T.psA[:, :], T.IDN[:, :], T.vbf[:, :], start=True, stop=False)], k_I, s_A0, d_v)
-            t_P2 = pe([lambda: P.matmul(T.psA[:, :], T.IDN[:, :], T.vs1[:, :], start=False, stop=True)], s_v1)
         A1, B1 = T["A%d" % (n + 1)], T["B%d" % (n + 1)]
-        a_h = vec(lambda U=U, A1=A1, n=n: V.tensor_scalar(A1[:, :], U[:, :], T.acol[:, n:n + 1], None, Op.mult), u_h, v_ac)
-        b_h = sca(lambda U=U, B1=B1, n=n: S.activation(B1[:, :], U[:, :], AF.Copy, scale=T.bcol[:, n:n + 1]), u_h, v_bc)
+        x_ = [extract(k + h, U[:, 256 * h:256 * h + 256], c7s, u_h[h], v_c7) for h in (0, 1)]
+        b_h = [sca(lambda U=U, B1=B1, n=n, h=h: S.activation(B1[:, 256 * h:256 * h + 256], U[:, 256 * h:256 * h + 256], AF.Copy,
+                                                            scale=T.bcol[:, n + 1:n + 2]), u_h[h], v_bc) for h in (0, 1)]
+        scb = T["scl%d" % (n + 1)]
+        sc = [scan(scb[:, 0:64], k, x_[0], md4)]
+        a_h = [vec(lambda U=U, A1=A1, n=n: V.tensor_scalar(A1[:, :], U[:, :], T.acol[:, n + 1:n + 2], None, Op.mult), *u_h, v_ac)]
+        sc.append(scan(scb[:, 64:128], k + 1, x_[1]))
+        l_h.append(vec(lambda n=n, scb=scb: V.tensor_copy(T["lst%d" % (n + 1)][:, :], scb[:, 3::4]), *sc))
+        bias(2 if n != 1 else 0, v_cv)
+        bias(3 if n != 1 else 1)
         if n == 0:
-            s_P2 = sca(lambda: S.activation(T.PT[:, 1024:1536], T.psA[:, :], AF.Copy), t_P2)
-            v_cv = vec(lambda: V.tensor_copy(T.CV[:, 3::4], T.SG[:, 3::4]), k_s2, mcv)
-        e_h.append(e_block(n, 32 if n < 2 else 16))
+            t_P = plus(2, 1, s_v1)
+            s_P2 = sca(lambda: S.activation(pt(2), sums[2][:, :], AF.Copy), t_P)
         if n == 1:
-            s_m = sca(lambda: S.activation(T.mabs[:, :], T.psE0[:, :], AF.Abs, bias=T.nicol[:, 0:1]), e_h[0], v_ni)
-            msk[0] = sca(lambda: S.activation(T.mask[:, 0:512], T.mabs[:, :], AF.Relu, bias=1.0, scale=-1.0), s_m)
-        sc = scan(T["scl%d" % (n + 1)], T.D2, bb, tl)
-        l_h.append(cvt(T["lst%d" % (n + 1)], T["scl%d" % (n + 1)], 2, sc))
+            s_v2 = sca(lambda: S.activation(T.vs2[:, :], T.vbf[:, :].indirect(T.lst1[:, :]), AF.Copy), l_h[1])
+            e_block(0, 0, 8)
+            plus(3, 1)
+        if n == 2:
+            t_P = plus(3, 2, s_v2)
+            e_block(0, 8, 16)
+            s_v3 = sca(lambda: S.activation(T.vs3[:, :], T.vs1[:, :].indirect(T.lst1[:, :]), AF.Copy), l_h[1])
+            s_P3 = sca(lambda: S.activation(pt(3), sums[3][:, :], AF.Copy), t_P)
+            plus(4, 0, s_P2)
+            plus(4, 1)
+            plus(4, 2)
+            t_P = plus(4, 3, s_v3)
     w_h = u_h
-
     for t in (1, 2, 3, 4):
-        send((rank - t) % NR, T["Wl%d" % t][:, :], T.W[:, :], "w%d" % t, [w_h])
+        send((rank - t) % NR, T["Wl%d" % t][:, :], T.W[:, :], "w%d" % t, w_h)
 
-    pt_h = {0: s_z, 1: s_P1, 2: s_P2}
+    pt_h = {2: s_P2, 3: s_P3}
+    q_h = {}
 
-    def slot(k):
-        if k == 16:
-            return T.P4[:, :]
-        return T.PT[:, 512 * k:512 * k + 512]
-
-    def build_add(k, frm, m, plus):
+    def move(e, frm, m):
         L = T["lst%d" % m]
-        pt_h[k] = vec(lambda: V.tensor_tensor(slot(k), slot(frm).indirect(L[:, :]), slot(plus), Op.add), pt_h[frm], pt_h[plus], l_h[m])
+        src, d = (T.vbf[:, :], d_v) if frm == 1 else (pt(frm), pt_h[frm])
+        pt_h[e] = sca(lambda: S.activation(pt(e), src.indirect(L[:, :]), AF.Copy), d, l_h[m])
 
-    def build_move(k, frm, m):
-        L = T["lst%d" % m]
-        pt_h[k] = sca(lambda: S.activation(slot(k), slot(frm).indirect(L[:, :]), AF.Copy), pt_h[frm], l_h[m])
+    def build_add(e, m, plus_e, h):
+        L, o, i = T["lst%d" % m], 512 * (3 - e // 4) + 256 * h, 512 * (3 - plus_e // 4) + 256 * h
+        q_h[e, h] = vec(lambda: V.tensor_tensor(T.TT[:, o:o + 256], T.P4[:, :].indirect(L[:, 16 * h:16 * h + 16]), T.TT[:, i:i + 256],
+                                                Op.add), *([s_P4, d_P4] if plus_e == 4 else [q_h[plus_e, h], d_P4]), l_h[m])
 
-    x_h = {}
+    msk = {}
 
-    def index(t):
-        c = 32 * t
-        if t == 0:
-            src, E, deps, rem = T.x128[:, :], T.Ecat, [d_x, v_e1, v_e2], []
+    def mask(t, n, *deps):
+        h = vec(lambda: V.tensor_scalar(T.mask[:, 256 * t:256 * (t + n)], T["psE%d" % (t // 2)][:, 256 * (t % 2):256 * (t % 2 + n)],
+                                        T.icol[:, 0:1], None, Op.is_equal), *deps)
+        for i in range(t, t + n):
+            msk[i] = h
+
+    v_ic = vec(lambda: V.tensor_copy(T.icol[:, :], T.ci[:, 1:2]), v_ci)
+    v_x = vec(lambda: V.tensor_copy(T.pl0[:, :], T.x128[:, :]), d_x)
+    mask(0, 1, e_h[0], e_h[1], v_ic)
+    x_h, E_h = {}, []
+
+    def expo():
+        a = vec(lambda: V.tensor_scalar(T.ea[:, :], T.EL[:, :], 2, None, Op.logical_shift_right), d_e0, rem=[("earr", n_arr)])
+        i1 = vec(lambda: V.tensor_scalar(T.E1[:, :], T.EL[:, :], 512.0, None, Op.mult), d_e0)
+        E_h.extend([i1, vec(lambda: V.tensor_scalar(T.E2[:, :], T.ea[:, :], -512.0, 1536.0, Op.mult, Op.add), a)])
+        E_h.append(vec(lambda: V.tensor_copy(T.QL[:, 3:64:4], T.x128[:, :]), d_x))
+
+    def index(lo, hi):
+        c = slice(16 * lo, 16 * hi + 16)
+        src, rem = T.QL[:, 64 * lo + 3:64 * hi + 64:4], [("rq%d" % t, n_arr) for t in range(max(lo, 1), hi + 1)]
+        i1 = vec(lambda: V.tensor_tensor(T.xf1[:, c], src, T.E1[:, c], Op.add), *E_h, rem=rem)
+        i2 = vec(lambda: V.tensor_tensor(T.xf2[:, c], src, T.E2[:, c], Op.add))
+        x1 = vec(lambda: V.tensor_copy(T.xi1[:, c], T.xf1[:, c]), i1)
+        x2 = vec(lambda: V.tensor_copy(T.xi2[:, c], T.xf2[:, c]), i2)
+        for t in range(lo, hi + 1):
+            x_h[t] = [x1, x2]
+
+    r_1, r_2 = {}, {}
+
+    def term(t, which, on):
+        w = T.TT[:, 1536:9728] if which == 1 else T.TT[:, 0:2048]
+        i = w.indirect(T["xi%d" % which][:, 16 * t:16 * t + 16])
+        deps = [x_h[t][which - 1]] + ([z_h[0], s_P4] + [q_h[e, h] for e in (8, 12) for h in (0, 1)] if which == 2 else
+                                      [*z_h, *pt_h.values()])
+        r, o = T["r1_%d" % t], T["rr%d" % t]
+        if t not in r_1:
+            r_1[t] = (sca(lambda: S.activation(r[:, :], i, AF.Copy), *deps) if on == "s" else
+                      vec(lambda: V.tensor_copy(r[:, :], i), *deps))
         else:
-            src, E = T["ql%d" % t][:, 3::4], T["el%d" % t]
-            deps, rem = [], [("earr", 5 * n_arr), ("rq%d" % t, n_arr)]
-        i1 = vec(lambda: V.tensor_tensor(T.xf[:, c:c + 16], src, E[:, 16 * t:16 * t + 16], Op.add), *deps, rem=rem)
-        i2 = vec(lambda: V.tensor_tensor(T.xf[:, c + 16:c + 32], src, E[:, 96 + 16 * t:112 + 16 * t], Op.add), *deps)
-        x_h[t] = vec(lambda: V.tensor_copy(T.xi[:, c:c + 32], T.xf[:, c:c + 32]), i1, i2)
+            r_2[t] = vec(lambda: V.tensor_tensor(o[:, :], i, r[:, :], Op.add), r_1[t], *deps)
+            if t:
+                send((rank - t) % NR, T["rl%d" % t][:, :], o[:, :], "rs%d" % t, [r_2[t]])
 
     p_h = {0: v_x}
-    build_move(5, 1, 2)
-    build_move(9, 1, 3)
-    build_move(13, 5, 3)
     for t in range(5):
         Wt = T.W if t == 0 else T["Wl%d" % t]
-        R, pl = T["R%d" % t], T["pl%d" % t]
+        R, pl, k = T["R%d" % t], T["pl%d" % t], (2 + t) % 4
         r_h = vec(lambda R=R, Wt=Wt, pl=pl, t=t: V.tensor_tensor(R[:, :], Wt[:, :].indirect(pl[:, :]), T.mask[:, 256 * t:256 * t + 256],
                                                                   Op.mult),
-                  w_h, p_h[t], msk[t // 2], rem=[("w%d" % t, n_arr)] if t else [])
-        bb, hb = bias(T.bV, k_bV)
-        tl = extract(bb, R, cvs, r_h, v_cv)
+                  *w_h, p_h[t], msk[t], rem=[("w%d" % t, n_arr)] if t else [])
+        tl = extract(k, R, cvs, r_h, v_cv)
         if t == 0:
-            build_move(6, 2, 2)
-            build_move(10, 2, 3)
+            e_block(1, 0, 16)
+        if t in (0, 1, 2):
+            bias((4 + t) % 4)
+        if t == 0:
+            move(5, 1, 2)
+            move(9, 1, 3)
+            s_P4 = sca(lambda: S.activation(slot(2), sums[4][:, :], AF.Copy), t_P)
+            d_P4 = add("y", lambda: Y.dma_start(T.P4[:, :], slot(2)), [s_P4], step=16)
+            for e, frm, m in ((13, 5, 3), (6, 2, 2), (10, 2, 3), (14, 6, 3), (7, 3, 2), (11, 3, 3), (15, 7, 3)):
+                move(e, frm, m)
+            mask(1, 1)
         elif t == 1:
-            msk[2] = e_mask(2, 16, e_h[2])
-            build_add(8, 4, 2, 16)
+            mask(2, 1, e_h[2])
+            e_block(2, 0, 16, s_P3)
         elif t == 2:
-            build_add(12, 8, 2, 4)
-            index(0)
-        elif t == 3:
-            index(1)
-        elif t == 4:
-            index(2)
+            mask(3, 1, e_h[2])
+            mask(4, 1, e_h[3])
+        else:
+            build_add(8, 2, 4, t - 3)
         scb = T["scv%d" % (t + 1)]
-        sc = scan(scb, T.D4, bb, tl, md4)
+        sc = scan(scb[:, :], k, tl, md4)
         if t < 4:
-            p_h[t + 1] = cvt(T["pl%d" % (t + 1)], scb, 4, sc)
-        send((rank + t + 1) % NR, T["ql%d" % (t + 1)][:, :], scb[:, :], "rq%d" % (t + 1), [sc])
+            p_h[t + 1] = vec(lambda t=t, scb=scb: V.tensor_copy(T["pl%d" % (t + 1)][:, :], scb[:, 3::4]), sc)
+        send((rank + t + 1) % NR, T.QL[:, 64 * (t + 1):64 * (t + 2)], scb[:, :], "rq%d" % (t + 1), [sc])
         if t == 0:
-            msk[1] = e_mask(1, 32, e_h[1])
-            build_add(3, 1, 1, 2)
-            build_add(4, 3, 0, 1)
-            pt_h[16] = sca(lambda: S.activation(slot(16), slot(4), AF.Copy), pt_h[4])
-            build_move(14, 6, 3)
-            build_move(7, 3, 2)
-            build_move(11, 3, 3)
-            build_move(15, 7, 3)
+            pt_h[1] = add("g", lambda: g.dma_start(pt(1), T.vbf[:, :]), [d_v], step=16)
+            expo()
 
-    all_pt = [pt_h[k] for k in range(16)]
-    r1 = {}
-
-    def first(t):
-        c, r = 32 * t, T["r1_%d" % t]
-        r1[t] = sca(lambda: S.activation(r[:, :], T.PT[:, :].indirect(T.xi[:, c:c + 16]), AF.Copy), x_h[t], *all_pt)
-
-    def second(t):
-        c, r = 32 * t, T["r1_%d" % t]
-        o = T["rr%d" % t] if t else T.acc
-        h = vec(lambda: V.tensor_tensor(o[:, :], T.PT[:, 0:6656].indirect(T.xi[:, c + 16:c + 32]), r[:, :], Op.add), r1[t], x_h[t])
-        if t:
-            send((rank - t) % NR, T["rl%d" % t][:, :], T["rr%d" % t][:, :], "rs%d" % t, [h])
-        return h
-
-    first(1)
-    first(2)
-    second(1)
-    index(3)
-    first(3)
-    second(2)
-    index(4)
-    first(4)
-    second(3)
-    first(0)
-    index(5)
-    first(5)
-    second(4)
-    second(5)
-    acc = second(0)
-    for t in range(1, 6):
-        o = T.psA[:, 0:256] if t < 5 else T.yb[:, :]
-        a = T.acc[:, :] if t == 1 else T.psA[:, 0:256]
-        acc = vec(lambda t=t, o=o, a=a: V.tensor_tensor(o, a, T["rl%d" % t][:, :], Op.add), acc, rem=[("rs%d" % t, n_arr)])
+    build_add(12, 3, 8, 0)
+    build_add(12, 3, 8, 1)
+    index(0, 2)
+    term(1, 1, "s")
+    term(2, 1, "s")
+    term(0, 2, "v")
+    term(1, 2, "v")
+    index(3, 4)
+    term(2, 2, "v")
+    term(4, 2, "s")
+    index(5, 5)
+    term(3, 1, "s")
+    term(5, 1, "s")
+    term(4, 1, "v")
+    term(3, 2, "v")
+    term(5, 2, "v")
+    term(0, 1, "v")
+    acc = vec(lambda: V.tensor_tensor(T.psE0[:, 0:256], T.rr0[:, :], T.rl1[:, :], Op.add), r_2[0], rem=[("rs1", n_arr)])
+    for t in (2, 4, 3, 5):
+        o = T.psE0[:, 0:256] if t != 5 else T.yb[:, :]
+        acc = vec(lambda o=o, t=t: V.tensor_tensor(o, T.psE0[:, 0:256], T["rl%d" % t][:, :], Op.add), acc, rem=[("rs%d" % t, n_arr)])
     d_y = add("y", lambda: Y.dma_start(T.y[:, :], T.yb[:, :]), [acc], step=16)
     add("y", [], [d_y])
 

@@ -6,10 +6,11 @@ NR = 6
 NPOOL = 110
 BF, F32, I32, U16 = "bfloat16", "float32", "int32", "uint16"
 SCRATCH = {}
-for _n, _c, _d in (("nx32", 128, I32), ("nxb", 128, BF), ("nxl", 32, I32), ("nxt", 32, I32), ("e128", 96, I32), ("ebf", 96, BF),
-                   ("e32b", 384, BF), ("x128", 16, I32), ("vbf", 512, BF), ("ones", 512, BF), ("c256", 64, BF), ("G32", 512, BF),
-                   ("Gb", 512, BF), ("CV", 144, BF), ("C7t", 144, BF), ("C7", 144, BF), ("L16", 128, BF), ("bVt", 64, BF),
-                   ("bV", 64, BF), ("IDN", 128, BF), ("D4", 64, F32), ("pc", 2, I32), ("ci", 2, I32), ("bt", 4, I32),
+for _n, _c, _d in (("nx16", 256, I32), ("nxb", 256, BF), ("nxl", 32, I32), ("nxt", 32, I32), ("e128", 96, I32), ("ebf", 96, BF),
+                   ("e16b", 768, BF), ("x128", 16, I32), ("vbf", 512, BF), ("ones", 256, BF), ("c256", 64, BF), ("o15", 256, BF),
+                   ("G16", 256, BF), ("Gb", 256, BF), ("ID1", 128, BF), ("idr", 512, BF),
+                   ("CV", 144, BF), ("C7", 144, BF), ("L4", 128, BF), ("bV", 64, BF), ("IDN", 128, BF), ("IDF", 128, F32),
+                   ("D4", 64, F32), ("pc", 2, I32), ("ci", 2, I32), ("bt", 4, I32),
                    ("icol", 1, F32), ("n15", 1, F32), ("acol", 4, F32), ("bcol", 4, F32), ("EL", 96, I32), ("ea", 96, I32),
                    ("E1", 96, F32), ("E2", 96, F32), ("QL", 384, F32), ("xf1", 96, F32), ("xi1", 96, U16), ("xf2", 96, F32),
                    ("xi2", 96, U16), ("W", 512, BF), ("mask", 1280, BF), ("TT", 9728, F32), ("P4", 512, F32), ("yb", 256, F32)):
@@ -57,7 +58,13 @@ def rank_program(g, core, T, topo):
     def gp(fn, *deps):
         return add("g", fn, deps)
 
-    d_nx = add("y", lambda: Y.dma_start(T.nx32[0:32, :], T.nx[:, :]), step=16)
+    def slot(k):
+        return T.TT[:, 512 * k:512 * k + 512]
+
+    def pt(e):
+        return slot(3 + e)
+
+    d_nx = add("y", lambda: Y.dma_start(T.nx16[0:16, :], T.nx[:, :]), step=16)
     d_l = [add("s", lambda: S.dma_start(T.nxl[:, 0:16], T.nx[0::2, :]), step=16),
            add("y", lambda: Y.dma_start(T.nxl[:, 16:32], T.nx[1::2, :]), step=16)]
     d_e = add("s", lambda: S.dma_start(T.e128[:, :], T.e[:, :]), step=16)
@@ -65,51 +72,39 @@ def rank_program(g, core, T, topo):
     d_e0 = add("y", lambda: Y.dma_start(T.EL[:, 0:16], T.e[:, 0:16]), step=16)
     d_x = add("y", lambda: Y.dma_start(T.x128[:, :], T.x[:, :]), step=16)
 
-    m1 = vec(lambda: V.memset(T.ones[:, :], 1.0))
-    m2 = vec(lambda: V.memset(T.c256[:, :], 256.0))
-    m_b = vec(lambda: V.memset(T.Gb[:, :], 0.0))
-    m_n = vec(lambda: V.memset(T.nxb[:, :], 0.0))
-    m_bs = [vec(lambda: V.memset(T.Gb[32:33, 15::16], 1.0), m_b)]
-    for q in (0, 1, 3):
-        m_bs.append(vec(lambda q=q: V.memset(T.Gb[64:65, 128 * q + 15:128 * q + 128:16], 128.0 * q - 256.0), m_b))
-    m_n1 = vec(lambda: V.memset(T.nxb[64:65, :], 1.0), m_n)
-    m_n2 = vec(lambda: V.tensor_tensor_scan(T.nxb[32:33, :], T.ones[32:33, 0:128], T.ones[32:33, 0:128], -1.0, Op.mult, Op.add),
-               m_n, m1)
     k_pc = gp(lambda: g.iota(T.pc[:, :], [[1, 2]], 0, 1))
-    k_G = gp(lambda: g.affine_select(T.G32[0:32, :], T.ones[0:32, :], [[-1, 4], [-4, 8], [0, 16]], Op.is_equal, 0.0, 0, 1), m1)
-    k_c7 = gp(lambda: g.affine_select(T.C7t[:, :], T.ones[:, 0:144], [[-16, 9], [0, 16]], Op.is_equal, 0.0, -7, 1))
-    k_L16 = gp(lambda: g.affine_select(T.L16[0:16, :], T.ones[0:16, 0:128], [[0, 8], [-1, 16]], Op.is_equal, 0.0, 0, 1))
-    k_I = gp(lambda: g.affine_select(T.IDN[:, :], T.ones[:, 0:128], [[-1, 128]], Op.is_equal, 0.0, 0, 1))
-    k_v1 = gp(lambda: g.affine_select(T.bVt[0:16, :], T.c256[0:16, :], [[0, 16], [-4, 4]], Op.is_ge, -2048.0, 0, 1), m2)
-    k_bV = gp(lambda: g.affine_select(T.bV[0:16, :], T.bVt[0:16, :], [[0, 16], [4, 4]], Op.is_ge, -2048.0, 3, -1), k_v1)
-    t_cv = pe([lambda: P.matmul(T.psL3[:, 0:128], T.G32[0:32, 0:128], T.G32[0:32, 0:128], start=True, stop=True)], k_G)
-
-    def slot(k):
-        return T.TT[:, 512 * k:512 * k + 512]
-
-    def pt(e):
-        return slot(3 + e)
-
-    z_h = [sca(lambda a=a: S.activation(pt(4 * a), T.ones[:, :], AF.Copy, scale=0.0), m1) for a in range(4)]
+    m_o = vec(lambda: V.memset(T.o15[0:16, :], 1.0))
+    m_o = vec(lambda: V.memset(T.o15[0:16, 15::16], 0.0), m_o)
+    k_Gb = gp(lambda: g.affine_select(T.Gb[0:16, :], T.o15[0:16, :], [[-1, 2], [-2, 8], [0, 16]], Op.is_equal, 0.0, 0, 1), m_o)
+    s_id = sca(lambda: S.activation(T.ID1[0:1, :], T.o15[0:1, 0:128], AF.Copy, bias=1.0, scale=-1.0), m_o)
+    m1 = vec(lambda: V.memset(T.ones[:, :], 1.0))
     v_ci = vec(lambda: V.tensor_scalar(T.ci[:, :], T.pc[:, :], 15, None, Op.bitwise_and), k_pc)
+    v_bt = [vec(lambda n=n: V.tensor_scalar(T.bt[:, n:n + 1], T.pc[:, 0:1], n, 1, Op.logical_shift_right, Op.bitwise_and), k_pc)
+            for n in range(2)]
     v_n15 = vec(lambda: V.tensor_scalar(T.n15[:, :], T.ci[:, 1:2], 1.0, None, Op.is_ge), v_ci)
-    v_bt = [vec(lambda n=n: V.tensor_scalar(T.bt[:, n:n + 1], T.ci[:, 0:1], n, 1, Op.logical_shift_right, Op.bitwise_and), v_ci)
-            for n in range(4)]
-    md4 = vec(lambda: V.memset(T.D4[:, :], 1.0))
-    mc7 = vec(lambda: V.memset(T.C7[:, :], 0.0))
-    mcv = vec(lambda: V.memset(T.CV[:, :], 0.0))
-    md4 = vec(lambda: V.memset(T.D4[:, 0::4], 0.0), md4)
+    v_r0 = vec(lambda: V.tensor_tensor_scan(T.idr[0:1, 0:256], T.ones[0:1, :], T.ones[0:1, :], -257.0, Op.mult, Op.add), m1)
+    v_bt += [vec(lambda n=n: V.tensor_scalar(T.bt[:, n:n + 1], T.pc[:, 0:1], n, 1, Op.logical_shift_right, Op.bitwise_and), k_pc)
+             for n in range(2, 4)]
     v_ac = vec(lambda: V.tensor_scalar(T.acol[:, :], T.bt[:, :], T.n15[:, 0:1], None, Op.mult), v_n15, *v_bt)
-    v_b = vec(lambda: V.tensor_copy(T.Gb[0:32, :], T.G32[0:32, :]), k_G, m_b)
-    v_b = vec(lambda: V.memset(T.Gb[0:32, 15::16], 0.0), v_b)
+    s_c256 = sca(lambda: S.activation(T.c256[0:4, :], T.ones[0:4, 0:64], AF.Copy, bias=256.0, scale=0.0), m1)
+    s_D4 = sca(lambda: S.activation(T.D4[:, :], T.ones[:, 0:64], AF.Copy), m1)
+    s_c7 = sca(lambda: S.activation(T.C7[:, :], T.ones[:, 0:144], AF.Copy, scale=0.0), m1)
+    s_D4 = sca(lambda: S.activation(T.D4[:, 0::4], T.ones[:, 0:16], AF.Copy, scale=0.0), s_D4)
+    s_r1 = sca(lambda: S.activation(T.idr[0:1, 256:512], T.idr[0:1, 0:256], AF.Copy, bias=256.0), v_r0)
+    s_G = sca(lambda: S.activation(T.G16[0:16, :], T.Gb[0:16, :], AF.Copy), k_Gb)
     v_bc = sca(lambda: S.activation(T.bcol[:, :], T.acol[:, :], AF.Copy, bias=1.0, scale=-1.0), v_ac)
+    k_I = gp(lambda: g.affine_select(T.IDN[:, :], T.ones[:, 0:128], [[-1, 128]], Op.is_equal, 0.0, 0, 1), m1)
+    k_L4 = gp(lambda: g.affine_select(T.L4[0:4, :], T.ones[0:4, 0:128], [[0, 8], [-1, 4], [0, 4]], Op.is_equal, 0.0, 0, 1), m1)
+    k_bV = gp(lambda: g.affine_select(T.bV[0:4, :], T.c256[0:4, :], [[0, 16], [-1, 4]], Op.is_equal, -2048.0, 0, 1), s_c256)
+    s_c7 = [sca(lambda q=q: S.activation(T.C7[:, 4 * q + 3:128:16], T.IDN[:, 7::16], AF.Copy), k_I, s_c7) for q in range(4)]
+    s_G = sca(lambda: S.activation(T.G16[0:16, 15::16], T.Gb[0:16, 14::16], AF.Copy), s_G)
 
     c7s = [T.C7[:, 3 - s:131 - s] for s in range(4)]
     cvs = [T.CV[:, 3 - s:131 - s] for s in range(4)]
 
     def bias(k, *deps):
         b = T["psL%d" % k]
-        pe([lambda: P.matmul(b[:, 0:64], T.L16[0:16, :], T.bV[0:16, :], start=True, stop=False)], *deps)
+        pe([lambda: P.matmul(b[:, 0:64], T.L4[0:4, :], T.bV[0:4, :], start=True, stop=False)], *deps)
 
     def extract(k, rows, cls, *deps):
         b = T["psL%d" % k]
@@ -118,20 +113,20 @@ def rank_program(g, core, T, topo):
     def scan(out, k, *deps):
         return vec(lambda: V.tensor_tensor_scan(out, T.D4[:, :], T["psL%d" % k][:, 0:64], 0.0, Op.mult, Op.max), *deps)
 
-    v_nx = vec(lambda: V.tensor_scalar(T.nxb[0:32, :], T.nx32[0:32, :], -256.0, None, Op.add), d_nx, m_n)
-    t_0 = [pe([lambda q=q: P.matmul(T["psE%d" % (q // 2)][:, 128 * (q % 2):128 * (q % 2) + 128], T.Gb[0:65, 128 * q:128 * q + 128],
-                                    T.nxb[0:65, :], start=True, stop=True) for q in (2 * h, 2 * h + 1)],
-              v_nx, v_b, m_n1, m_n2, *m_bs) for h in (0, 1)]
-    v_tr = vec(lambda: V.transpose(T.nxt[:, :], T.nxl[:, :]), *d_l)
-    v_l0 = vec(lambda: V.tensor_copy(T.lst0[:, :], T.nxt[:, :]), v_tr)
-    s_A0 = sca(lambda: S.activation(T.A0[:, 0:256], T.psE0[:, 0:256], AF.Copy, scale=T.acol[:, 0:1]), t_0[0], v_ac)
+    v_nx = vec(lambda: V.tensor_scalar(T.nxb[0:16, :], T.nx16[0:16, :], -256.0, None, Op.add), d_nx)
+    for h in (0, 1):
+        pe([lambda h=h: P.matmul(T["psE%d" % h][:, 0:256], T.ID1[0:1, :], T.idr[0:1, 256 * h:256 * h + 256], start=True, stop=False)],
+           s_id, v_r0, *([s_r1] if h else []))
+    t_0 = [pe([lambda h=h: P.matmul(T["psE%d" % h][:, 0:256], T.Gb[0:16, 128 * h:128 * h + 128], T.nxb[0:16, :], start=False, stop=True)],
+              v_nx, k_Gb) for h in (0, 1)]
     v_eb = vec(lambda: V.tensor_copy(T.ebf[:, :], T.e128[:, :]), d_e)
-    d_8 = add("y", lambda: Y.dma_start(T.e32b[0:32, :], T.ebf[:, :]), [v_eb], step=16)
+    d_8 = add("y", lambda: Y.dma_start(T.e16b[0:16, :], T.ebf[:, :]), [v_eb], step=16)
+    v_tr = vec(lambda: V.transpose(T.nxt[:, :], T.nxl[:, :]), *d_l)
+    s_A0 = sca(lambda: S.activation(T.A0[:, 0:256], T.psE0[:, 0:256], AF.Copy, scale=T.acol[:, 0:1]), t_0[0], v_ac)
+    v_l0 = vec(lambda: V.tensor_copy(T.lst0[:, :], T.nxt[:, :]), v_tr)
     v_A0 = vec(lambda: V.tensor_scalar(T.A0[:, 256:512], T.psE1[:, 0:256], T.acol[:, 0:1], None, Op.mult), t_0[1], v_ac)
     v_B0 = vec(lambda: V.tensor_scalar(T.B0[:, 0:256], T.psE0[:, 0:256], T.bcol[:, 0:1], None, Op.mult), s_A0, v_bc)
     s_B0 = sca(lambda: S.activation(T.B0[:, 256:512], T.psE1[:, 0:256], AF.Copy, scale=T.bcol[:, 0:1]), v_A0, v_bc)
-    v_c7 = sca(lambda: S.activation(T.C7[:, 3::4], T.C7t[:, 3::4], AF.Copy), k_c7, mc7)
-    v_cv = sca(lambda: S.activation(T.CV[:, 3:128:4], T.psL3[:, 3:128:4], AF.Copy), t_cv, mcv)
 
     loc = [0]
 
@@ -155,27 +150,32 @@ def rank_program(g, core, T, topo):
                                         srcs=[T.e128[:, 16 * t:16 * t + 16]], dsts=[T.EL[:, 16 * t:16 * t + 16]]), n))
     loc[0] += n_arr
     add("g", lambda: g.remote_dma_fused([p[0] for p in parts], local_sem=T.sem.loc), [d_e], step=0)
+    z_h = []
+
+    def zero(a):
+        z_h.append(gp(lambda: g.iota(pt(4 * a), [[0, 512]], 0, 0, allow_small_or_imprecise_dtypes=True)))
+
+    zero(0)
 
     s_v1 = sca(lambda: S.activation(T.vs1[:, :], T.vbf[:, :].indirect(T.lst0[:, :]), AF.Copy), v_l0, d_v)
-    sums = {2: T.psT, 3: T.psE2, 4: T.psT}
     vs = [T.vbf, T.vs1, T.vs2, T.vs3]
 
     def plus(k, i, *deps):
-        return pe([lambda: P.matmul(sums[k][:, :], T.IDN[:, :], vs[i][:, :], start=(i == 0), stop=(i == k - 1))], *deps)
+        return pe([lambda: P.matmul(T.psT[:, :], T.IDN[:, :], vs[i][:, :], start=(i == 0), stop=(i == k - 1))], *deps)
 
-    plus(2, 0, k_I, d_v)
-    plus(3, 0)
-    bias(0, k_L16, k_bV)
+    bias(0, k_L4, k_bV)
     bias(1)
+    plus(2, 0, k_I, d_v)
+    t_cv = pe([lambda: P.matmul(T.psL3[:, 0:128], T.G16[0:16, 0:128], T.G16[0:16, 0:128], start=True, stop=True)], s_G)
     l_h = [v_l0]
     a_h, b_h = [s_A0, v_A0], [v_B0, s_B0]
     e_h = []
 
     def e_block(u, lo, hi, *deps):
         ps, w = T["psE%d" % u], 32 if u < 2 else 16
-        e_h.append(pe([lambda i=i: P.matmul(ps[:, i:16 * w:16], T.G32[0:32, 128 * (i // 4):128 * (i // 4) + 128],
-                                            T.e32b[0:32, 96 * (i % 4) + 32 * u:96 * (i % 4) + 32 * u + w], start=True, stop=True)
-                       for i in range(lo, hi)], d_8, k_G, s_B0, v_B0, *deps))
+        e_h.append(pe([lambda i=i: P.matmul(ps[:, i:16 * w:16], T.G16[0:16, 128 * (i // 8):128 * (i // 8) + 128],
+                                            T.e16b[0:16, 96 * (i % 8) + 32 * u:96 * (i % 8) + 32 * u + w], start=True, stop=True)
+                       for i in range(lo, hi)], d_8, s_G, s_B0, v_B0, *deps))
 
     for n in range(4):
         A, B, L = T["A%d" % n], T["B%d" % n], T["lst%d" % n]
@@ -188,37 +188,42 @@ def rank_program(g, core, T, topo):
         if n == 3:
             break
         A1, B1 = T["A%d" % (n + 1)], T["B%d" % (n + 1)]
-        x_ = [extract(k + h, U[:, 256 * h:256 * h + 256], c7s, u_h[h], v_c7) for h in (0, 1)]
+        x_ = [extract(k + h, U[:, 256 * h:256 * h + 256], c7s, u_h[h], *s_c7) for h in (0, 1)]
         b_h = [sca(lambda U=U, B1=B1, n=n, h=h: S.activation(B1[:, 256 * h:256 * h + 256], U[:, 256 * h:256 * h + 256], AF.Copy,
                                                             scale=T.bcol[:, n + 1:n + 2]), u_h[h], v_bc) for h in (0, 1)]
         scb = T["scl%d" % (n + 1)]
-        sc = [scan(scb[:, 0:64], k, x_[0], md4)]
+        sc = [scan(scb[:, 0:64], k, x_[0], s_D4)]
         a_h = [vec(lambda U=U, A1=A1, n=n: V.tensor_scalar(A1[:, :], U[:, :], T.acol[:, n + 1:n + 2], None, Op.mult), *u_h, v_ac)]
         sc.append(scan(scb[:, 64:128], k + 1, x_[1]))
         l_h.append(vec(lambda n=n, scb=scb: V.tensor_copy(T["lst%d" % (n + 1)][:, :], scb[:, 3::4]), *sc))
-        bias(2 if n != 1 else 0, v_cv)
-        bias(3 if n != 1 else 1)
         if n == 0:
+            k_cv = sca(lambda: S.activation(T.CV[:, :], T.C7[:, :], AF.Copy, scale=0.0), *s_c7)
+            k_cv = sca(lambda: S.activation(T.CV[:, 3:128:4], T.psL3[:, 3:128:4], AF.Copy), k_cv, t_cv)
+            bias(2)
             t_P = plus(2, 1, s_v1)
-            s_P2 = sca(lambda: S.activation(pt(2), sums[2][:, :], AF.Copy), t_P)
+            s_P2 = sca(lambda: S.activation(pt(2), T.psT[:, :], AF.Copy), t_P)
+            y_P3 = add("y", lambda: Y.dma_start(pt(3), pt(2)), [s_P2], step=16)
+            bias(3, k_cv)
+            e_block(0, 0, 4)
         if n == 1:
+            bias(0)
+            bias(1)
             s_v2 = sca(lambda: S.activation(T.vs2[:, :], T.vbf[:, :].indirect(T.lst1[:, :]), AF.Copy), l_h[1])
-            e_block(0, 0, 8)
-            plus(3, 1)
+            e_block(0, 4, 12)
         if n == 2:
-            t_P = plus(3, 2, s_v2)
-            e_block(0, 8, 16)
+            bias(2)
+            bias(3)
             s_v3 = sca(lambda: S.activation(T.vs3[:, :], T.vs1[:, :].indirect(T.lst1[:, :]), AF.Copy), l_h[1])
-            s_P3 = sca(lambda: S.activation(pt(3), sums[3][:, :], AF.Copy), t_P)
+            e_block(0, 12, 16)
+            e_block(1, 0, 16)
             plus(4, 0, s_P2)
-            plus(4, 1)
-            plus(4, 2)
-            t_P = plus(4, 3, s_v3)
     w_h = u_h
     for t in (1, 2, 3, 4):
         send((rank - t) % NR, T["Wl%d" % t][:, :], T.W[:, :], "w%d" % t, w_h)
 
-    pt_h = {2: s_P2, 3: s_P3}
+    pt_h = {2: s_P2}
+    pt_h[3] = add("g", lambda: g.dma_start(pt(3), T.vs2[:, :], accum_op=Op.add), [y_P3, s_v2], step=16)
+    zero(1)
     q_h = {}
 
     def move(e, frm, m):
@@ -233,15 +238,13 @@ def rank_program(g, core, T, topo):
 
     msk = {}
 
-    def mask(t, n, *deps):
-        h = vec(lambda: V.tensor_scalar(T.mask[:, 256 * t:256 * (t + n)], T["psE%d" % (t // 2)][:, 256 * (t % 2):256 * (t % 2 + n)],
-                                        T.icol[:, 0:1], None, Op.is_equal), *deps)
-        for i in range(t, t + n):
-            msk[i] = h
+    def mask(t, *deps):
+        msk[t] = vec(lambda: V.tensor_scalar(T.mask[:, 256 * t:256 * t + 256], T["psE%d" % (t // 2)][:, 256 * (t % 2):256 * (t % 2) + 256],
+                                             T.icol[:, 0:1], None, Op.is_equal), *deps)
 
     v_ic = vec(lambda: V.tensor_copy(T.icol[:, :], T.ci[:, 1:2]), v_ci)
     v_x = vec(lambda: V.tensor_copy(T.pl0[:, :], T.x128[:, :]), d_x)
-    mask(0, 1, e_h[0], e_h[1], v_ic)
+    mask(0, e_h[2], v_ic)
     x_h, E_h = {}, []
 
     def expo():
@@ -272,7 +275,8 @@ def rank_program(g, core, T, topo):
             r_1[t] = (sca(lambda: S.activation(r[:, :], i, AF.Copy), *deps) if on == "s" else
                       vec(lambda: V.tensor_copy(r[:, :], i), *deps))
         else:
-            r_2[t] = vec(lambda: V.tensor_tensor(o[:, :], i, r[:, :], Op.add), r_1[t], *deps)
+            r_2[t] = (sca(lambda: S.activation(o[:, :], i, AF.Copy), *deps) if on == "s" else
+                      vec(lambda: V.tensor_tensor(o[:, :], i, r[:, :], Op.add), r_1[t], *deps))
             if t:
                 send((rank - t) % NR, T["rl%d" % t][:, :], o[:, :], "rs%d" % t, [r_2[t]])
 
@@ -283,55 +287,64 @@ def rank_program(g, core, T, topo):
         r_h = vec(lambda R=R, Wt=Wt, pl=pl, t=t: V.tensor_tensor(R[:, :], Wt[:, :].indirect(pl[:, :]), T.mask[:, 256 * t:256 * t + 256],
                                                                   Op.mult),
                   *w_h, p_h[t], msk[t], rem=[("w%d" % t, n_arr)] if t else [])
-        tl = extract(k, R, cvs, r_h, v_cv)
-        if t == 0:
-            e_block(1, 0, 16)
+        tl = extract(k, R, cvs, r_h, k_cv)
         if t in (0, 1, 2):
             bias((4 + t) % 4)
         if t == 0:
-            move(5, 1, 2)
-            move(9, 1, 3)
-            s_P4 = sca(lambda: S.activation(slot(2), sums[4][:, :], AF.Copy), t_P)
-            d_P4 = add("y", lambda: Y.dma_start(T.P4[:, :], slot(2)), [s_P4], step=16)
-            for e, frm, m in ((13, 5, 3), (6, 2, 2), (10, 2, 3), (14, 6, 3), (7, 3, 2), (11, 3, 3), (15, 7, 3)):
+            plus(4, 1)
+            plus(4, 2, s_v2)
+            t_P = plus(4, 3, s_v3)
+            for e, frm, m in ((5, 1, 2), (6, 2, 2), (9, 1, 3)):
                 move(e, frm, m)
-            mask(1, 1)
+            s_P4 = sca(lambda: S.activation(slot(2), T.psT[:, :], AF.Copy), t_P)
+            d_P4 = add("y", lambda: Y.dma_start(T.P4[:, :], slot(2)), [s_P4], step=16)
+            for e, frm, m in ((13, 5, 3), (10, 2, 3), (14, 6, 3)):
+                move(e, frm, m)
+            pt_h[1] = sca(lambda: S.activation(pt(1), T.vbf[:, :], AF.Copy), d_v)
+            for e, frm, m in ((7, 3, 2), (11, 3, 3), (15, 7, 3)):
+                move(e, frm, m)
+            mask(1, e_h[3])
         elif t == 1:
-            mask(2, 1, e_h[2])
-            e_block(2, 0, 16, s_P3)
+            e_block(2, 0, 8)
+            mask(3, e_h[3])
         elif t == 2:
-            mask(3, 1, e_h[2])
-            mask(4, 1, e_h[3])
+            e_block(2, 8, 16)
+            expo()
+        elif t == 3:
+            mask(4, e_h[5])
         else:
-            build_add(8, 2, 4, t - 3)
+            build_add(8, 2, 4, 0)
         scb = T["scv%d" % (t + 1)]
-        sc = scan(scb[:, :], k, tl, md4)
+        sc = scan(scb[:, :], k, tl, s_D4)
         if t < 4:
             p_h[t + 1] = vec(lambda t=t, scb=scb: V.tensor_copy(T["pl%d" % (t + 1)][:, :], scb[:, 3::4]), sc)
         send((rank + t + 1) % NR, T.QL[:, 64 * (t + 1):64 * (t + 2)], scb[:, :], "rq%d" % (t + 1), [sc])
+        if t < 2:
+            zero(t + 2)
         if t == 0:
-            pt_h[1] = add("g", lambda: g.dma_start(pt(1), T.vbf[:, :]), [d_v], step=16)
-            expo()
+            mask(2, e_h[3])
 
-    build_add(12, 3, 8, 0)
-    build_add(12, 3, 8, 1)
-    index(0, 2)
+    index(0, 3)
     term(1, 1, "s")
+    build_add(8, 2, 4, 1)
+    build_add(12, 3, 8, 0)
     term(2, 1, "s")
-    term(0, 2, "v")
-    term(1, 2, "v")
-    index(3, 4)
-    term(2, 2, "v")
-    term(4, 2, "s")
-    index(5, 5)
+    term(0, 1, "s")
+    build_add(12, 3, 8, 1)
+    v_If = vec(lambda: V.tensor_copy(T.IDF[:, :], T.IDN[:, :]), k_I)
     term(3, 1, "s")
+    term(1, 2, "v")
+    index(4, 5)
+    term(2, 2, "v")
+    term(4, 1, "s")
     term(5, 1, "s")
-    term(4, 1, "v")
     term(3, 2, "v")
+    term(4, 2, "v")
     term(5, 2, "v")
-    term(0, 1, "v")
-    acc = vec(lambda: V.tensor_tensor(T.psE0[:, 0:256], T.rr0[:, :], T.rl1[:, :], Op.add), r_2[0], rem=[("rs1", n_arr)])
-    for t in (2, 4, 3, 5):
+    term(0, 2, "s")
+    acc = pe([lambda: P.matmul(T.psE0[:, 0:256], T.IDF[:, :], T.r1_0[:, :], start=True, stop=False)], r_1[0], v_If)
+    acc = pe([lambda: P.matmul(T.psE0[:, 0:256], T.IDF[:, :], T.rr0[:, :], start=False, stop=True)], r_2[0])
+    for t in (1, 2, 3, 4, 5):
         o = T.psE0[:, 0:256] if t != 5 else T.yb[:, :]
         acc = vec(lambda o=o, t=t: V.tensor_tensor(o, T.psE0[:, 0:256], T["rl%d" % t][:, :], Op.add), acc, rem=[("rs%d" % t, n_arr)])
     d_y = add("y", lambda: Y.dma_start(T.y[:, :], T.yb[:, :]), [acc], step=16)

import numpy as np
from concourse.bass import DstId, RemoteDMATransfer
from concourse.mybir import dt, AluOpType, AxisListType, ActivationFunctionType

NR = 6
NPOOL = 110
BF, F32, I32, U16 = "bfloat16", "float32", "int32", "uint16"
SCRATCH = {}
for _n, _c, _d in (("nx16", 256, I32), ("nxb", 256, BF), ("nxl", 32, I32), ("nxt", 32, I32), ("e128", 96, I32), ("ebf", 96, BF),
                   ("e16b", 768, BF), ("x128", 16, I32), ("vbf", 512, BF), ("ones", 256, BF), ("c256", 64, BF), ("o15", 256, BF),
                   ("G16", 256, BF), ("Gb", 256, BF), ("ID1", 128, BF), ("idr", 512, BF),
                   ("CV", 144, BF), ("C7", 144, BF), ("L4", 128, BF), ("bV", 64, BF), ("IDN", 128, BF), ("IDF", 128, F32),
                   ("D4", 64, F32), ("pc", 2, I32), ("ci", 2, I32), ("bt", 4, I32),
                   ("icol", 1, F32), ("n15", 1, F32), ("acol", 4, F32), ("bcol", 4, F32), ("EL", 96, I32), ("ea", 96, I32),
                   ("E1", 96, F32), ("E2", 96, F32), ("QL", 384, F32), ("xf1", 96, F32), ("xi1", 96, U16), ("xf2", 96, F32),
                   ("xi2", 96, U16), ("W", 512, BF), ("mask", 1280, BF), ("TT", 9728, F32), ("P4", 512, F32), ("yb", 256, F32)):
    SCRATCH[_n] = ("sbuf", [128, _c], _d)
for _n in range(6):
    for _b, _c, _d, _k in (("A", 512, BF, (0, 1, 2, 3)), ("B", 512, BF, (0, 1, 2, 3)), ("U", 512, BF, (1, 2, 3)),
                           ("vs", 512, BF, (1, 2, 3)), ("scl", 128, F32, (1, 2, 3)), ("lst", 32, U16, (0, 1, 2, 3)),
                           ("Wl", 512, BF, (1, 2, 3, 4)), ("r1_", 256, F32, range(6)), ("rr", 256, F32, range(6)),
                           ("pl", 16, U16, range(5)), ("R", 256, BF, range(5)), ("scv", 64, F32, range(1, 6)),
                           ("rl", 256, F32, range(1, 6))):
        if _n in _k:
            SCRATCH["%s%d" % (_b, _n)] = ("sbuf", [128, _c], _d)
for _n in ("psL0", "psL1", "psL2", "psL3", "psE0", "psE1", "psE2", "psT"):
    SCRATCH[_n] = ("psum", [128, 512], F32)

SEMAPHORES = (["s%d" % k for k in range(NPOOL)] + ["loc", "earr"] + ["w%d" % k for k in range(1, 5)]
              + ["rq%d" % k for k in range(1, 6)] + ["rs%d" % k for k in range(1, 6)])


def rank_program(g, core, T, topo):
    rank = T.rank_of(core)
    if rank is None:
        return
    queues = {"g": g, "v": g.vector, "s": g.scalar, "t": g.tensor, "y": g.sync}
    ops = []
    Op, AF = AluOpType, ActivationFunctionType

    def add(q, calls, deps=(), rem=(), step=1):
        if not isinstance(calls, list):
            calls = [calls]
        ops.append((q, calls, list(deps), list(rem), step))
        return len(ops) - 1

    V, S, P, Y = g.vector, g.scalar, g.tensor, g.sync

    def vec(fn, *deps, rem=()):
        return add("v", fn, deps, rem)

    def sca(fn, *deps, rem=()):
        return add("s", fn, deps, rem)

    def pe(fns, *deps):
        return add("t", fns, deps)

    def gp(fn, *deps):
        return add("g", fn, deps)

    def slot(k):
        return T.TT[:, 512 * k:512 * k + 512]

    def pt(e):
        return slot(3 + e)

    d_nx = add("y", lambda: Y.dma_start(T.nx16[0:16, :], T.nx[:, :]), step=16)
    d_l = [add("s", lambda: S.dma_start(T.nxl[:, 0:16], T.nx[0::2, :]), step=16),
           add("y", lambda: Y.dma_start(T.nxl[:, 16:32], T.nx[1::2, :]), step=16)]
    d_e = add("s", lambda: S.dma_start(T.e128[:, :], T.e[:, :]), step=16)
    d_v = add("s", lambda: S.dma_start(T.vbf[:, :], T.v[:, :]), step=16)
    d_e0 = add("y", lambda: Y.dma_start(T.EL[:, 0:16], T.e[:, 0:16]), step=16)
    d_x = add("y", lambda: Y.dma_start(T.x128[:, :], T.x[:, :]), step=16)

    k_pc = gp(lambda: g.iota(T.pc[:, :], [[1, 2]], 0, 1))
    m_o = vec(lambda: V.memset(T.o15[0:16, :], 1.0))
    m_o = vec(lambda: V.memset(T.o15[0:16, 15::16], 0.0), m_o)
    k_Gb = gp(lambda: g.affine_select(T.Gb[0:16, :], T.o15[0:16, :], [[-1, 2], [-2, 8], [0, 16]], Op.is_equal, 0.0, 0, 1), m_o)
    s_id = sca(lambda: S.activation(T.ID1[0:1, :], T.o15[0:1, 0:128], AF.Copy, bias=1.0, scale=-1.0), m_o)
    m1 = vec(lambda: V.memset(T.ones[:, :], 1.0))
    v_ci = vec(lambda: V.tensor_scalar(T.ci[:, :], T.pc[:, :], 15, None, Op.bitwise_and), k_pc)
    v_bt = [vec(lambda n=n: V.tensor_scalar(T.bt[:, n:n + 1], T.pc[:, 0:1], n, 1, Op.logical_shift_right, Op.bitwise_and), k_pc)
            for n in range(2)]
    v_n15 = vec(lambda: V.tensor_scalar(T.n15[:, :], T.ci[:, 1:2], 1.0, None, Op.is_ge), v_ci)
    v_r0 = vec(lambda: V.tensor_tensor_scan(T.idr[0:1, 0:256], T.ones[0:1, :], T.ones[0:1, :], -257.0, Op.mult, Op.add), m1)
    v_bt += [vec(lambda n=n: V.tensor_scalar(T.bt[:, n:n + 1], T.pc[:, 0:1], n, 1, Op.logical_shift_right, Op.bitwise_and), k_pc)
             for n in range(2, 4)]
    v_ac = vec(lambda: V.tensor_scalar(T.acol[:, :], T.bt[:, :], T.n15[:, 0:1], None, Op.mult), v_n15, *v_bt)
    s_c256 = sca(lambda: S.activation(T.c256[0:4, :], T.ones[0:4, 0:64], AF.Copy, bias=256.0, scale=0.0), m1)
    s_D4 = sca(lambda: S.activation(T.D4[:, :], T.ones[:, 0:64], AF.Copy), m1)
    s_c7 = sca(lambda: S.activation(T.C7[:, :], T.ones[:, 0:144], AF.Copy, scale=0.0), m1)
    s_D4 = sca(lambda: S.activation(T.D4[:, 0::4], T.ones[:, 0:16], AF.Copy, scale=0.0), s_D4)
    s_r1 = sca(lambda: S.activation(T.idr[0:1, 256:512], T.idr[0:1, 0:256], AF.Copy, bias=256.0), v_r0)
    s_G = sca(lambda: S.activation(T.G16[0:16, :], T.Gb[0:16, :], AF.Copy), k_Gb)
    v_bc = sca(lambda: S.activation(T.bcol[:, :], T.acol[:, :], AF.Copy, bias=1.0, scale=-1.0), v_ac)
    k_I = gp(lambda: g.affine_select(T.IDN[:, :], T.ones[:, 0:128], [[-1, 128]], Op.is_equal, 0.0, 0, 1), m1)
    k_L4 = gp(lambda: g.affine_select(T.L4[0:4, :], T.ones[0:4, 0:128], [[0, 8], [-1, 4], [0, 4]], Op.is_equal, 0.0, 0, 1), m1)
    k_bV = gp(lambda: g.affine_select(T.bV[0:4, :], T.c256[0:4, :], [[0, 16], [-1, 4]], Op.is_equal, -2048.0, 0, 1), s_c256)
    s_c7 = [sca(lambda q=q: S.activation(T.C7[:, 4 * q + 3:128:16], T.IDN[:, 7::16], AF.Copy), k_I, s_c7) for q in range(4)]
    s_G = sca(lambda: S.activation(T.G16[0:16, 15::16], T.Gb[0:16, 14::16], AF.Copy), s_G)

    c7s = [T.C7[:, 3 - s:131 - s] for s in range(4)]
    cvs = [T.CV[:, 3 - s:131 - s] for s in range(4)]

    def bias(k, *deps):
        b = T["psL%d" % k]
        pe([lambda: P.matmul(b[:, 0:64], T.L4[0:4, :], T.bV[0:4, :], start=True, stop=False)], *deps)

    def extract(k, rows, cls, *deps):
        b = T["psL%d" % k]
        return pe([lambda s=s: P.matmul(b[:, 0:64], cls[s], rows[:, s::4], start=False, stop=(s == 3)) for s in range(4)], *deps)

    def scan(out, k, *deps):
        return vec(lambda: V.tensor_tensor_scan(out, T.D4[:, :], T["psL%d" % k][:, 0:64], 0.0, Op.mult, Op.max), *deps)

    v_nx = vec(lambda: V.tensor_scalar(T.nxb[0:16, :], T.nx16[0:16, :], -256.0, None, Op.add), d_nx)
    for h in (0, 1):
        pe([lambda h=h: P.matmul(T["psE%d" % h][:, 0:256], T.ID1[0:1, :], T.idr[0:1, 256 * h:256 * h + 256], start=True, stop=False)],
           s_id, v_r0, *([s_r1] if h else []))
    t_0 = [pe([lambda h=h: P.matmul(T["psE%d" % h][:, 0:256], T.Gb[0:16, 128 * h:128 * h + 128], T.nxb[0:16, :], start=False, stop=True)],
              v_nx, k_Gb) for h in (0, 1)]
    v_eb = vec(lambda: V.tensor_copy(T.ebf[:, :], T.e128[:, :]), d_e)
    d_8 = add("y", lambda: Y.dma_start(T.e16b[0:16, :], T.ebf[:, :]), [v_eb], step=16)
    v_tr = vec(lambda: V.transpose(T.nxt[:, :], T.nxl[:, :]), *d_l)
    s_A0 = sca(lambda: S.activation(T.A0[:, 0:256], T.psE0[:, 0:256], AF.Copy, scale=T.acol[:, 0:1]), t_0[0], v_ac)
    v_l0 = vec(lambda: V.tensor_copy(T.lst0[:, :], T.nxt[:, :]), v_tr)
    v_A0 = vec(lambda: V.tensor_scalar(T.A0[:, 256:512], T.psE1[:, 0:256], T.acol[:, 0:1], None, Op.mult), t_0[1], v_ac)
    v_B0 = vec(lambda: V.tensor_scalar(T.B0[:, 0:256], T.psE0[:, 0:256], T.bcol[:, 0:1], None, Op.mult), s_A0, v_bc)
    s_B0 = sca(lambda: S.activation(T.B0[:, 256:512], T.psE1[:, 0:256], AF.Copy, scale=T.bcol[:, 0:1]), v_A0, v_bc)

    loc = [0]

    def eng(d):
        return len(topo.engines(core, d))

    n_arr = eng([c for c in T.cores if c != core][0])

    def send(dst_rank, out, in_, sem, deps):
        d = T.cores[dst_rank]
        rid, pid, _ = topo.addr(d)
        loc[0] += eng(d)
        add("g", lambda: g.remote_dma(out, in_, T.sem[sem], T.sem.loc, pid, rid, topo.mask(core, d)), deps, step=0)

    parts, es = [], topo.engines(core, [c for c in T.cores if c != core][0])
    for t in range(1, NR):
        d, n = T.cores[(rank + t) % NR], len(es) // (4 if t < 4 else 8)
        o = sum(p[1] for p in parts)
        parts.append((RemoteDMATransfer(dst_ids=[DstId(rid=topo.addr(d)[0], pnc=topo.addr(d)[1])],
                                        dma_engine_mask=sum(1 << x for x in es[o:o + n]), remote_sem=T.sem["earr"],
                                        srcs=[T.e128[:, 16 * t:16 * t + 16]], dsts=[T.EL[:, 16 * t:16 * t + 16]]), n))
    loc[0] += n_arr
    add("g", lambda: g.remote_dma_fused([p[0] for p in parts], local_sem=T.sem.loc), [d_e], step=0)
    z_h = []

    def zero(a):
        z_h.append(gp(lambda: g.iota(pt(4 * a), [[0, 512]], 0, 0, allow_small_or_imprecise_dtypes=True)))

    zero(0)

    s_v1 = sca(lambda: S.activation(T.vs1[:, :], T.vbf[:, :].indirect(T.lst0[:, :]), AF.Copy), v_l0, d_v)
    vs = [T.vbf, T.vs1, T.vs2, T.vs3]

    def plus(k, i, *deps):
        return pe([lambda: P.matmul(T.psT[:, :], T.IDN[:, :], vs[i][:, :], start=(i == 0), stop=(i == k - 1))], *deps)

    bias(0, k_L4, k_bV)
    bias(1)
    plus(2, 0, k_I, d_v)
    t_cv = pe([lambda: P.matmul(T.psL3[:, 0:128], T.G16[0:16, 0:128], T.G16[0:16, 0:128], start=True, stop=True)], s_G)
    l_h = [v_l0]
    a_h, b_h = [s_A0, v_A0], [v_B0, s_B0]
    e_h = []

    def e_block(u, lo, hi, *deps):
        ps, w = T["psE%d" % u], 32 if u < 2 else 16
        e_h.append(pe([lambda i=i: P.matmul(ps[:, i:16 * w:16], T.G16[0:16, 128 * (i // 8):128 * (i // 8) + 128],
                                            T.e16b[0:16, 96 * (i % 8) + 32 * u:96 * (i % 8) + 32 * u + w], start=True, stop=True)
                       for i in range(lo, hi)], d_8, s_G, s_B0, v_B0, *deps))

    for n in range(4):
        A, B, L = T["A%d" % n], T["B%d" % n], T["lst%d" % n]
        U = T["U%d" % (n + 1)] if n < 3 else T.W
        k = 2 * (n % 2)
        u_h = [vec(lambda A=A, B=B, U=U, L=L, h=h: V.tensor_tensor(U[:, 256 * h:256 * h + 256],
                                                                  A[:, :].indirect(L[:, 16 * h:16 * h + 16]),
                                                                  B[:, 256 * h:256 * h + 256], Op.add),
                   *a_h, b_h[h], l_h[n]) for h in (0, 1)]
        if n == 3:
            break
        A1, B1 = T["A%d" % (n + 1)], T["B%d" % (n + 1)]
        x_ = [extract(k + h, U[:, 256 * h:256 * h + 256], c7s, u_h[h], *s_c7) for h in (0, 1)]
        b_h = [sca(lambda U=U, B1=B1, n=n, h=h: S.activation(B1[:, 256 * h:256 * h + 256], U[:, 256 * h:256 * h + 256], AF.Copy,
                                                            scale=T.bcol[:, n + 1:n + 2]), u_h[h], v_bc) for h in (0, 1)]
        scb = T["scl%d" % (n + 1)]
        sc = [scan(scb[:, 0:64], k, x_[0], s_D4)]
        a_h = [vec(lambda U=U, A1=A1, n=n: V.tensor_scalar(A1[:, :], U[:, :], T.acol[:, n + 1:n + 2], None, Op.mult), *u_h, v_ac)]
        sc.append(scan(scb[:, 64:128], k + 1, x_[1]))
        l_h.append(vec(lambda n=n, scb=scb: V.tensor_copy(T["lst%d" % (n + 1)][:, :], scb[:, 3::4]), *sc))
        if n == 0:
            k_cv = sca(lambda: S.activation(T.CV[:, :], T.C7[:, :], AF.Copy, scale=0.0), *s_c7)
            k_cv = sca(lambda: S.activation(T.CV[:, 3:128:4], T.psL3[:, 3:128:4], AF.Copy), k_cv, t_cv)
            bias(2)
            t_P = plus(2, 1, s_v1)
            s_P2 = sca(lambda: S.activation(pt(2), T.psT[:, :], AF.Copy), t_P)
            y_P3 = add("y", lambda: Y.dma_start(pt(3), pt(2)), [s_P2], step=16)
            bias(3, k_cv)
            e_block(0, 0, 4)
        if n == 1:
            bias(0)
            bias(1)
            s_v2 = sca(lambda: S.activation(T.vs2[:, :], T.vbf[:, :].indirect(T.lst1[:, :]), AF.Copy), l_h[1])
            e_block(0, 4, 12)
        if n == 2:
            bias(2)
            bias(3)
            s_v3 = sca(lambda: S.activation(T.vs3[:, :], T.vs1[:, :].indirect(T.lst1[:, :]), AF.Copy), l_h[1])
            e_block(0, 12, 16)
            e_block(1, 0, 16)
            plus(4, 0, s_P2)
    w_h = u_h
    for t in (1, 2, 3, 4):
        send((rank - t) % NR, T["Wl%d" % t][:, :], T.W[:, :], "w%d" % t, w_h)

    pt_h = {2: s_P2}
    pt_h[3] = add("g", lambda: g.dma_start(pt(3), T.vs2[:, :], accum_op=Op.add), [y_P3, s_v2], step=16)
    zero(1)
    q_h = {}

    def move(e, frm, m):
        L = T["lst%d" % m]
        src, d = (T.vbf[:, :], d_v) if frm == 1 else (pt(frm), pt_h[frm])
        pt_h[e] = sca(lambda: S.activation(pt(e), src.indirect(L[:, :]), AF.Copy), d, l_h[m])

    def build_add(e, m, plus_e, h):
        L, o, i = T["lst%d" % m], 512 * (3 - e // 4) + 256 * h, 512 * (3 - plus_e // 4) + 256 * h
        q_h[e, h] = vec(lambda: V.tensor_tensor(T.TT[:, o:o + 256], T.P4[:, :].indirect(L[:, 16 * h:16 * h + 16]), T.TT[:, i:i + 256],
                                                Op.add), *([s_P4, d_P4] if plus_e == 4 else [q_h[plus_e, h], d_P4]), l_h[m])

    msk = {}

    def mask(t, *deps):
        msk[t] = vec(lambda: V.tensor_scalar(T.mask[:, 256 * t:256 * t + 256], T["psE%d" % (t // 2)][:, 256 * (t % 2):256 * (t % 2) + 256],
                                             T.icol[:, 0:1], None, Op.is_equal), *deps)

    v_ic = vec(lambda: V.tensor_copy(T.icol[:, :], T.ci[:, 1:2]), v_ci)
    v_x = vec(lambda: V.tensor_copy(T.pl0[:, :], T.x128[:, :]), d_x)
    mask(0, e_h[2], v_ic)
    x_h, E_h = {}, []

    def expo():
        a = vec(lambda: V.tensor_scalar(T.ea[:, :], T.EL[:, :], 2, None, Op.logical_shift_right), d_e0, rem=[("earr", n_arr)])
        i1 = vec(lambda: V.tensor_scalar(T.E1[:, :], T.EL[:, :], 512.0, None, Op.mult), d_e0)
        E_h.extend([i1, vec(lambda: V.tensor_scalar(T.E2[:, :], T.ea[:, :], -512.0, 1536.0, Op.mult, Op.add), a)])
        E_h.append(vec(lambda: V.tensor_copy(T.QL[:, 3:64:4], T.x128[:, :]), d_x))

    def index(lo, hi):
        c = slice(16 * lo, 16 * hi + 16)
        src, rem = T.QL[:, 64 * lo + 3:64 * hi + 64:4], [("rq%d" % t, n_arr) for t in range(max(lo, 1), hi + 1)]
        i1 = vec(lambda: V.tensor_tensor(T.xf1[:, c], src, T.E1[:, c], Op.add), *E_h, rem=rem)
        i2 = vec(lambda: V.tensor_tensor(T.xf2[:, c], src, T.E2[:, c], Op.add))
        x1 = vec(lambda: V.tensor_copy(T.xi1[:, c], T.xf1[:, c]), i1)
        x2 = vec(lambda: V.tensor_copy(T.xi2[:, c], T.xf2[:, c]), i2)
        for t in range(lo, hi + 1):
            x_h[t] = [x1, x2]

    r_1, r_2 = {}, {}

    def term(t, which, on):
        w = T.TT[:, 1536:9728] if which == 1 else T.TT[:, 0:2048]
        i = w.indirect(T["xi%d" % which][:, 16 * t:16 * t + 16])
        deps = [x_h[t][which - 1]] + ([z_h[0], s_P4] + [q_h[e, h] for e in (8, 12) for h in (0, 1)] if which == 2 else
                                      [*z_h, *pt_h.values()])
        r, o = T["r1_%d" % t], T["rr%d" % t]
        if t not in r_1:
            r_1[t] = (sca(lambda: S.activation(r[:, :], i, AF.Copy), *deps) if on == "s" else
                      vec(lambda: V.tensor_copy(r[:, :], i), *deps))
        else:
            r_2[t] = (sca(lambda: S.activation(o[:, :], i, AF.Copy), *deps) if on == "s" else
                      vec(lambda: V.tensor_tensor(o[:, :], i, r[:, :], Op.add), r_1[t], *deps))
            if t:
                send((rank - t) % NR, T["rl%d" % t][:, :], o[:, :], "rs%d" % t, [r_2[t]])

    p_h = {0: v_x}
    for t in range(5):
        Wt = T.W if t == 0 else T["Wl%d" % t]
        R, pl, k = T["R%d" % t], T["pl%d" % t], (2 + t) % 4
        r_h = vec(lambda R=R, Wt=Wt, pl=pl, t=t: V.tensor_tensor(R[:, :], Wt[:, :].indirect(pl[:, :]), T.mask[:, 256 * t:256 * t + 256],
                                                                  Op.mult),
                  *w_h, p_h[t], msk[t], rem=[("w%d" % t, n_arr)] if t else [])
        tl = extract(k, R, cvs, r_h, k_cv)
        if t in (0, 1, 2):
            bias((4 + t) % 4)
        if t == 0:
            plus(4, 1)
            plus(4, 2, s_v2)
            t_P = plus(4, 3, s_v3)
            for e, frm, m in ((5, 1, 2), (6, 2, 2), (9, 1, 3)):
                move(e, frm, m)
            s_P4 = sca(lambda: S.activation(slot(2), T.psT[:, :], AF.Copy), t_P)
            d_P4 = add("y", lambda: Y.dma_start(T.P4[:, :], slot(2)), [s_P4], step=16)
            for e, frm, m in ((13, 5, 3), (10, 2, 3), (14, 6, 3)):
                move(e, frm, m)
            pt_h[1] = sca(lambda: S.activation(pt(1), T.vbf[:, :], AF.Copy), d_v)
            for e, frm, m in ((7, 3, 2), (11, 3, 3), (15, 7, 3)):
                move(e, frm, m)
            mask(1, e_h[3])
        elif t == 1:
            e_block(2, 0, 8)
            mask(3, e_h[3])
        elif t == 2:
            e_block(2, 8, 16)
            expo()
        elif t == 3:
            mask(4, e_h[5])
        else:
            build_add(8, 2, 4, 0)
        scb = T["scv%d" % (t + 1)]
        sc = scan(scb[:, :], k, tl, s_D4)
        if t < 4:
            p_h[t + 1] = vec(lambda t=t, scb=scb: V.tensor_copy(T["pl%d" % (t + 1)][:, :], scb[:, 3::4]), sc)
        send((rank + t + 1) % NR, T.QL[:, 64 * (t + 1):64 * (t + 2)], scb[:, :], "rq%d" % (t + 1), [sc])
        if t < 2:
            zero(t + 2)
        if t == 0:
            mask(2, e_h[3])

    index(0, 3)
    term(1, 1, "s")
    build_add(8, 2, 4, 1)
    build_add(12, 3, 8, 0)
    term(2, 1, "s")
    term(0, 1, "s")
    build_add(12, 3, 8, 1)
    v_If = vec(lambda: V.tensor_copy(T.IDF[:, :], T.IDN[:, :]), k_I)
    term(3, 1, "s")
    term(1, 2, "v")
    index(4, 5)
    term(2, 2, "v")
    term(4, 1, "s")
    term(5, 1, "s")
    term(3, 2, "v")
    term(4, 2, "v")
    term(5, 2, "v")
    term(0, 2, "s")
    acc = pe([lambda: P.matmul(T.psE0[:, 0:256], T.IDF[:, :], T.r1_0[:, :], start=True, stop=False)], r_1[0], v_If)
    acc = pe([lambda: P.matmul(T.psE0[:, 0:256], T.IDF[:, :], T.rr0[:, :], start=False, stop=True)], r_2[0])
    for t in (1, 2, 3, 4, 5):
        o = T.psE0[:, 0:256] if t != 5 else T.yb[:, :]
        acc = vec(lambda o=o, t=t: V.tensor_tensor(o, T.psE0[:, 0:256], T["rl%d" % t][:, :], Op.add), acc, rem=[("rs%d" % t, n_arr)])
    d_y = add("y", lambda: Y.dma_start(T.y[:, :], T.yb[:, :]), [acc], step=16)
    add("y", [], [d_y])

    known = {q: set() for q in queues}
    seen_rem = {q: set() for q in queues}
    waits, at_issue = [], []
    for k, (q, calls, deps, rem, step) in enumerate(ops):
        w = []
        for d in deps:
            if d not in known[q]:
                w.append(d)
                known[q] |= at_issue[d]
                known[q].add(d)
        w = [d for d in w if not any(d in at_issue[o] for o in w if o != d)]
        waits.append(w)
        at_issue.append(set(known[q]))
    wanted = set(d for w in waits for d in w)
    count, last, sem_of, owner = {}, {}, {}, {}
    free = list(range(NPOOL))
    for k, (q, calls, deps, rem, step) in enumerate(ops):
        eq = queues[q]
        for d in waits[k]:
            eq.wait_ge(T.sem["s%d" % sem_of[d][0]], sem_of[d][1])
        for name, val in rem:
            if name not in seen_rem[q]:
                eq.wait_ge(T.sem[name], val)
                seen_rem[q].add(name)
        if k in wanted:
            s = None
            if step == 1:
                for c in owner.get(q, []):
                    if last[c] in at_issue[k]:
                        s = c
                        break
            if s is None:
                s = free.pop(0)
                count[s] = 0
                if step == 1:
                    owner.setdefault(q, []).append(s)
            for fn in calls:
                fn().then_inc(T.sem["s%d" % s], step)
                count[s] += step
            last[s] = k
            sem_of[k] = (s, count[s])
        else:
            for fn in calls:
                fn()
    g.wait_ge(T.sem.loc, loc[0])
